import numpy as np
import ml_dtypes


def mxq(x, axis, fmt="e4m3"):
    dtype, down = {"e4m3": (ml_dtypes.float8_e4m3fn, 7), "e5m2": (ml_dtypes.float8_e5m2, 14)}[fmt]
    v = np.moveaxis(np.asarray(x, np.float32).astype(ml_dtypes.bfloat16).astype(np.float64), axis, -1)
    blocks = v.reshape(v.shape[:-1] + (-1, 32))
    amax = np.abs(blocks).max(-1, keepdims=True)
    byte = np.maximum(np.where(amax > 0, np.frexp(amax)[1] - 1 + 127, 0) - down, 1)
    scale = np.exp2(byte - 127.0)
    codes = (blocks / scale).astype(np.float32).astype(dtype).astype(np.float64)
    return np.moveaxis((codes * scale).reshape(v.shape), -1, axis)


WIDE = False


def mx_kscale(k):
    if not WIDE:
        return np.ones(k)
    levels = np.array([10, -10, 5, -5, 0])
    if k % 512:
        return np.exp2(np.random.permutation(np.resize(levels, k // 32))).repeat(32)
    a = np.empty((k // 512, 16))
    for p in range(k // 512):
        a[p, :8] = np.random.permutation(np.resize(levels, 8))
        for g in range(8):
            far = levels[np.abs(levels - a[p, g]) >= 10]
            a[p, g + 8] = far[np.random.randint(len(far))]
    return np.exp2(a.ravel()).repeat(32)


def f64(x):
    return np.asarray(x).astype(np.float64)


def striped8(idx):
    return np.concatenate([v.reshape(-1, 16).T for v in idx]).astype(np.uint16)


def unstriped8(offs):
    return np.stack([offs[16 * g:16 * g + 16].T.reshape(-1) for g in range(8)]).astype(np.int64)


def split(x):
    m, e = np.frexp(f64(x))
    hi = np.ldexp(np.trunc(16.0 * m) / 16.0, e)
    return hi, f64(x) - hi


def silu(v):
    return v / (1.0 + np.exp(-np.maximum(v, -700.0)))


K, M, T, S = 1536, 256, 1024, 512


def setup_inputs():
    n = np.random.standard_normal
    s = mx_kscale(K)[:, None]
    return {
        "xT": (n((K, T)) * s).astype(np.float32),
        "w": (n((K, M)) / np.sqrt(K) / s).astype(np.float32),
        "wgt": np.repeat(np.random.uniform(0.5, 2.0, (8, S)), 16, axis=0).astype(np.float32),
        "b": (0.3 * n(256)).astype(np.float32),
        "offs": striped8(np.stack([np.random.permutation(T)[:S] for _ in range(8)])),
    }


def reference(xT, w, wgt, b, offs):
    idx = unstriped8(offs)
    group = np.arange(K) % 512 // 64
    xg = f64(wgt)[np.arange(K) // 4 % 128] * f64(xT)[np.arange(K)[:, None], idx[group]]
    xT_ = mxq(xg, 0, "e4m3")
    w_hi, w_lo = split(w)
    w_hi_, w_lo_ = mxq(w_hi, 0, "e4m3"), mxq(w_lo, 0, "e4m3")
    y = xT_.T @ w_hi_ + xT_.T @ w_lo_
    return silu(y + f64(b)[None, :])

@@ -1,0 +1,213 @@
+from contextlib import ExitStack
+
+import concourse.mybir as mybir
+
+K, N, TOKENS, PICKS = 1536, 256, 1024, 512
+FLOPS = 2 * 2 * K * N * PICKS
+
+F32 = mybir.dt.float32
+BF16 = mybir.dt.bfloat16
+I32 = mybir.dt.int32
+U32 = mybir.dt.uint32
+U16 = mybir.dt.uint16
+U8 = mybir.dt.uint8
+FP8X4 = mybir.dt.float8_e4m3fn_x4
+ACT = mybir.ActivationFunctionType
+ALU = mybir.AluOpType
+
+P = 128
+PACK = 4
+K_PASS = P * PACK
+PASSES = K // K_PASS
+ROW_TILES = PICKS // P
+
+KEEP_HIGH_BITS = -0x000F0010
+
+
+def tile_list_heads_tm_hl_silu_kernel(tc, xT, w, wgt, b, offs, out):
+    nc = tc.nc
+
+    with ExitStack() as ctx:
+        keep = ctx.enter_context(tc.tile_pool(name="keep", bufs=1))
+        psum = ctx.enter_context(tc.psum_pool(name="psum", bufs=1))
+
+        def held(shape, dtype, name):
+            return keep.tile(shape, dtype, name=name, align_bytes=64)
+
+        offsets = keep.tile([P, PICKS // 16], U16, name="offsets")
+        weights = held([P, PICKS], F32, "weights")
+        bias = held([P, N], F32, "bias")
+        warm = held([P, 1], F32, "warm")
+        planes = [[held([P, TOKENS], F32, f"plane{a}_{i}") for i in range(PACK)] for a in range(PASSES)]
+        w_raw = [held([P, PACK, N], F32, f"w_raw{a}") for a in range(PASSES)]
+        w_top = [held([P, N, PACK], BF16, f"w_top{a}") for a in range(PASSES)]
+        grouped = [held([P, PICKS + 2 * N, PACK], BF16, f"grouped{a}") for a in range(PASSES)]
+        codes = [held([P, PICKS + 2 * N], U32, f"codes{a}") for a in range(PASSES)]
+        scales = [held([P, PICKS + 2 * N], U8, f"scales{a}") for a in range(PASSES)]
+        sums = [psum.tile([P, 512], F32, name=f"sums{t}") for t in range(ROW_TILES)]
+
+        def load_w(a):
+            nc.sync.dma_start(w_raw[a][:], w[a * K_PASS : (a + 1) * K_PASS, :].rearrange("(p i) n -> p i n", i=PACK))
+
+        def load_plane(a, i):
+            nc.sync.dma_start(
+                planes[a][i][:],
+                xT[a * K_PASS : (a + 1) * K_PASS, :].rearrange("(p i) t -> p i t", i=PACK)[:, i, :],
+            )
+
+        nc.vector.memset(warm[:], 0.0)
+        nc.scalar.activation(warm[:], warm[:], ACT.Silu)
+
+        nc.sync.dma_start(offsets[:], offs)
+        half = PICKS // 2
+        nc.sync.dma_start(weights[:, 0:half], wgt[:, 0:half])
+        load_plane(0, 0)
+        nc.sync.dma_start(weights[:, half:PICKS], wgt[:, half:PICKS])
+        for i in range(1, PACK):
+            load_plane(0, i)
+        load_w(0)
+        load_plane(1, 0)
+        load_plane(1, 1)
+        load_w(1)
+        load_plane(1, 2)
+        load_plane(1, 3)
+        load_w(2)
+        for i in range(PACK):
+            load_plane(2, i)
+        nc.sync.dma_start(bias[:], b.partition_broadcast(P))
+
+        HI, LO, END = PICKS, PICKS + N, PICKS + 2 * N
+
+        def by_rows(interleaved):
+            return interleaved.rearrange("p (c e) i -> p c i e", e=4)
+
+        def by_planes(separate):
+            return separate.rearrange("p i (c e) -> p c i e", e=4)
+
+        def truncate_w(a):
+            nc.scalar.copy(by_rows(w_top[a][:]), by_planes(w_raw[a][:].bitcast(BF16)[:, :, 1 : 2 * N : 2]))
+
+        def mask_w(a):
+            nc.vector.tensor_scalar(
+                grouped[a][:, HI:LO, :].rearrange("p n i -> p (n i)").bitcast(I32),
+                w_top[a][:].rearrange("p n i -> p (n i)").bitcast(I32),
+                KEEP_HIGH_BITS,
+                None,
+                ALU.bitwise_and,
+            )
+
+        def subtract_w(a):
+            nc.vector.tensor_tensor(
+                by_rows(grouped[a][:, LO:END, :]),
+                by_planes(w_raw[a][:]),
+                by_rows(grouped[a][:, HI:LO, :]),
+                ALU.subtract,
+            )
+
+        cuts = [((0, 256), (256, 512)), ((0, 256), (256, 512)), ((0, 384), (384, 512))]
+        picked = [
+            {lo: held([P, PACK, hi - lo], F32, f"picked{a}_{lo}") for lo, hi in cuts[a]} for a in range(PASSES)
+        ]
+
+        def gather(a, i, c):
+            lo, hi = cuts[a][c]
+            nc.vector.tensor_tensor(
+                picked[a][lo][:, i, :],
+                planes[a][i][:].indirect(offsets[:, lo // 16 : hi // 16]),
+                weights[:, lo:hi],
+                ALU.mult,
+            )
+
+        def interleave(a, c):
+            lo, hi = cuts[a][c]
+            nc.scalar.copy(by_rows(grouped[a][:, lo:hi, :]), by_planes(picked[a][lo][:]))
+
+        def interleave_last():
+            lo, hi = cuts[2][1]
+            mid = 448
+            source = picked[2][lo]
+            nc.scalar.copy(by_rows(grouped[2][:, mid:hi, :]), by_planes(source[:, :, mid - lo : hi - lo]))
+            nc.vector.tensor_copy(by_rows(grouped[2][:, lo:mid, :]), by_planes(source[:, :, 0 : mid - lo]))
+
+        def quantize(a, lo, hi):
+            nc.vector.quantize_mx(
+                out=codes[a][:, lo:hi].bitcast(FP8X4),
+                scales=scales[a][:, lo:hi],
+                in_=grouped[a][:, lo:hi, :].rearrange("p j i -> p (j i)"),
+            )
+
+        def multiply(a, t):
+            rows = slice(t * P, (t + 1) * P)
+            for h in range(2):
+                cols = slice(HI + h * N, LO + h * N)
+                nc.tensor.matmul_mx(
+                    out=sums[t][:, 0:N],
+                    lhsT=codes[a][:, rows].bitcast(FP8X4),
+                    lhsT_scale=scales[a][:, rows],
+                    rhs=codes[a][:, cols].bitcast(FP8X4),
+                    rhs_scale=scales[a][:, cols],
+                    start=(a == 0 and h == 0),
+                    stop=(a == PASSES - 1 and h == 1),
+                )
+
+        def finish(t):
+            shifted = keep.tile([P, N], F32, name=f"shifted{t}")
+            nc.vector.tensor_tensor(shifted[:], sums[t][:, 0:N], bias[:], ALU.add)
+            result = keep.tile([P, N], F32, name=f"result{t}")
+            nc.scalar.activation(result[:], shifted[:], ACT.Silu)
+            nc.sync.dma_start(out[t * P : (t + 1) * P, :], result[:])
+
+        def multiply_all(a):
+            for t in range(ROW_TILES):
+                multiply(a, t)
+
+        def gather_plane(a, i):
+            for c in range(2):
+                gather(a, i, c)
+
+        for i in range(PACK):
+            gather_plane(0, i)
+        truncate_w(0)
+        interleave(0, 0)
+        interleave(0, 1)
+        gather_plane(1, 0)
+        mask_w(0)
+        gather_plane(1, 1)
+        subtract_w(0)
+        truncate_w(1)
+        gather_plane(1, 2)
+        mask_w(1)
+        quantize(0, 0, END)
+        multiply_all(0)
+        gather_plane(1, 3)
+        subtract_w(1)
+        truncate_w(2)
+        interleave(1, 0)
+        interleave(1, 1)
+
+        gather(2, 0, 0)
+        mask_w(2)
+        gather(2, 1, 0)
+        subtract_w(2)
+        gather(2, 2, 0)
+        gather(2, 3, 0)
+        interleave(2, 0)
+        quantize(1, 0, END)
+        multiply_all(1)
+        gather(2, 0, 1)
+        quantize(2, HI, END)
+        gather(2, 1, 1)
+        gather(2, 2, 1)
+        quantize(2, 0, 256)
+        multiply(2, 0)
+        multiply(2, 1)
+        quantize(2, 256, 384)
+        multiply(2, 2)
+        gather(2, 3, 1)
+        finish(0)
+        interleave_last()
+        finish(1)
+        quantize(2, 384, 512)
+        multiply(2, 3)
+        finish(2)
+        finish(3)

@@ -1,6 +1,7 @@
 from contextlib import ExitStack
 
 import concourse.mybir as mybir
+from concourse.masks import make_identity
 
 K, N, TOKENS, PICKS = 1536, 256, 1024, 512
 FLOPS = 2 * 2 * K * N * PICKS
@@ -21,7 +22,8 @@ K_PASS = P * PACK
 PASSES = K // K_PASS
 ROW_TILES = PICKS // P
 
-KEEP_HIGH_BITS = -0x000F0010
+KEEP_HIGH_WORD = -0x00100000
+SIGN_BIT = -0x80000000
 
 
 def tile_list_heads_tm_hl_silu_kernel(tc, xT, w, wgt, b, offs, out):
@@ -35,12 +37,16 @@ def tile_list_heads_tm_hl_silu_kernel(tc, xT, w, wgt, b, offs, out):
             return keep.tile(shape, dtype, name=name, align_bytes=64)
 
         offsets = keep.tile([P, PICKS // 16], U16, name="offsets")
-        weights = held([P, PICKS], F32, "weights")
+        weights = held([P, PICKS + P], F32, "weights")
         bias = held([P, N], F32, "bias")
         warm = held([P, 1], F32, "warm")
         planes = [[held([P, TOKENS], F32, f"plane{a}_{i}") for i in range(PACK)] for a in range(PASSES)]
-        w_raw = [held([P, PACK, N], F32, f"w_raw{a}") for a in range(PASSES)]
-        w_top = [held([P, N, PACK], BF16, f"w_top{a}") for a in range(PASSES)]
+        w_raw = {a: held([P, PACK, N], F32, f"w_raw{a}") for a in (1, 2)}
+        w_first = [held([P, PACK, N // 2], F32, f"w_first{h}") for h in range(2)]
+        hi_first = [held([P, PACK, N // 2], F32, f"hi_first{h}") for h in range(2)]
+        minus_hi = {a: held([P, PACK, N], F32, f"minus_hi{a}") for a in (1, 2)}
+        lo_turned = {a: [held([P, 2, P, 2], BF16, f"lo_turned{a}_{h}") for h in range(2)] for a in (1, 2)}
+        identity = held([P, P], F32, "identity")
         grouped = [held([P, PICKS + 2 * N, PACK], BF16, f"grouped{a}") for a in range(PASSES)]
         codes = [held([P, PICKS + 2 * N], U32, f"codes{a}") for a in range(PASSES)]
         scales = [held([P, PICKS + 2 * N], U8, f"scales{a}") for a in range(PASSES)]
@@ -55,25 +61,26 @@ def tile_list_heads_tm_hl_silu_kernel(tc, xT, w, wgt, b, offs, out):
                 xT[a * K_PASS : (a + 1) * K_PASS, :].rearrange("(p i) t -> p i t", i=PACK)[:, i, :],
             )
 
+        make_identity(nc, identity[:])
         nc.vector.memset(warm[:], 0.0)
         nc.scalar.activation(warm[:], warm[:], ACT.Silu)
 
-        nc.sync.dma_start(offsets[:], offs)
-        half = PICKS // 2
-        nc.sync.dma_start(weights[:, 0:half], wgt[:, 0:half])
-        load_plane(0, 0)
-        nc.sync.dma_start(weights[:, half:PICKS], wgt[:, half:PICKS])
-        for i in range(1, PACK):
-            load_plane(0, i)
-        load_w(0)
-        load_plane(1, 0)
-        load_plane(1, 1)
+        for h in range(2):
+            nc.sync.dma_start(
+                w_first[h][:],
+                w[0:K_PASS, h * (N // 2) : (h + 1) * (N // 2)].rearrange("(p i) n -> p i n", i=PACK),
+            )
         load_w(1)
-        load_plane(1, 2)
-        load_plane(1, 3)
+        nc.sync.dma_start(offsets[:], offs)
+        nc.sync.dma_start(weights[:, 0:PICKS], wgt)
+        load_plane(0, 0)
+        load_plane(0, 1)
         load_w(2)
-        for i in range(PACK):
-            load_plane(2, i)
+        load_plane(0, 2)
+        load_plane(0, 3)
+        for a in (1, 2):
+            for i in range(PACK):
+                load_plane(a, i)
         nc.sync.dma_start(bias[:], b.partition_broadcast(P))
 
         HI, LO, END = PICKS, PICKS + N, PICKS + 2 * N
@@ -84,50 +91,83 @@ def tile_list_heads_tm_hl_silu_kernel(tc, xT, w, wgt, b, offs, out):
         def by_planes(separate):
             return separate.rearrange("p i (c e) -> p c i e", e=4)
 
-        def truncate_w(a):
-            nc.scalar.copy(by_rows(w_top[a][:]), by_planes(w_raw[a][:].bitcast(BF16)[:, :, 1 : 2 * N : 2]))
-
-        def mask_w(a):
+        def mask_words(hi, raw):
             nc.vector.tensor_scalar(
-                grouped[a][:, HI:LO, :].rearrange("p n i -> p (n i)").bitcast(I32),
-                w_top[a][:].rearrange("p n i -> p (n i)").bitcast(I32),
-                KEEP_HIGH_BITS,
+                hi.rearrange("p i n -> p (i n)").bitcast(I32),
+                raw.rearrange("p i n -> p (i n)").bitcast(I32),
+                KEEP_HIGH_WORD,
                 None,
                 ALU.bitwise_and,
             )
 
-        def subtract_w(a):
+        def upper_halves(words):
+            width = words.shape[2]
+            return by_planes(words.bitcast(BF16)[:, :, 1 : 2 * width : 2])
+
+        def weave_hi(a, hi, n0):
+            nc.scalar.copy(by_rows(grouped[a][:, HI + n0 : HI + n0 + hi.shape[2], :]), upper_halves(hi))
+
+        def subtract_words(a, raw, hi, n0):
             nc.vector.tensor_tensor(
-                by_rows(grouped[a][:, LO:END, :]),
-                by_planes(w_raw[a][:]),
-                by_rows(grouped[a][:, HI:LO, :]),
-                ALU.subtract,
+                by_rows(grouped[a][:, LO + n0 : LO + n0 + hi.shape[2], :]), by_planes(raw), by_planes(hi), ALU.subtract
             )
 
-        cuts = [((0, 256), (256, 512)), ((0, 256), (256, 512)), ((0, 384), (384, 512))]
-        picked = [
-            {lo: held([P, PACK, hi - lo], F32, f"picked{a}_{lo}") for lo, hi in cuts[a]} for a in range(PASSES)
-        ]
+        def split_w(a):
+            nc.vector.tensor_scalar(
+                minus_hi[a][:].rearrange("p i n -> p (i n)").bitcast(I32),
+                w_raw[a][:].rearrange("p i n -> p (i n)").bitcast(I32),
+                KEEP_HIGH_WORD,
+                SIGN_BIT,
+                ALU.bitwise_and,
+                ALU.bitwise_xor,
+            )
+            for h in range(2):
+                cols = slice(h * P, (h + 1) * P)
+                difference = psum.tile([P, PACK, P], F32, name=f"difference{h}")
+                for i in range(PACK):
+                    for term, source in enumerate((w_raw[a], minus_hi[a])):
+                        nc.tensor.matmul(
+                            difference[:, i, :],
+                            source[:, i, cols],
+                            identity[:],
+                            start=(term == 0),
+                            stop=(term == 1),
+                            is_transpose=True,
+                        )
+                nc.scalar.copy(lo_turned[a][h][:], difference[:].rearrange("n (u e) p -> n u p e", e=2))
+            back = psum.tile([P, 2, 2, P], F32, name="back")
+            for h in range(2):
+                words = lo_turned[a][h][:].rearrange("n u p e -> n u (p e)").bitcast(F32)
+                for u in range(2):
+                    nc.tensor.transpose(back[:, h, u, :], words[:, u, :], identity[:])
+            nc.scalar.copy(
+                grouped[a][:, LO:END, :].bitcast(F32).rearrange("p (h n) u -> p h n u", h=2),
+                back[:].rearrange("p h u n -> p h n u"),
+            )
 
-        def gather(a, i, c):
-            lo, hi = cuts[a][c]
+        def weave_minus_hi(a):
+            nc.scalar.activation(by_rows(grouped[a][:, HI:LO, :]), upper_halves(minus_hi[a][:]), ACT.Copy, scale=-1.0)
+
+        picked = [held([P, PACK, PICKS], F32, f"picked{a}") for a in range(2)]
+        picked_long = held([P, PACK, PICKS - P], F32, "picked_long")
+        picked_short = weights[:, P : PICKS + P].rearrange("p (i j) -> p i j", i=PACK)
+
+        def gather(into, a, i, lo, hi):
             nc.vector.tensor_tensor(
-                picked[a][lo][:, i, :],
+                into[:, i, :],
                 planes[a][i][:].indirect(offsets[:, lo // 16 : hi // 16]),
                 weights[:, lo:hi],
                 ALU.mult,
             )
 
-        def interleave(a, c):
-            lo, hi = cuts[a][c]
-            nc.scalar.copy(by_rows(grouped[a][:, lo:hi, :]), by_planes(picked[a][lo][:]))
+        def interleave(a):
+            nc.scalar.copy(by_rows(grouped[a][:, 0:PICKS, :]), by_planes(picked[a][:]))
 
-        def interleave_last():
-            lo, hi = cuts[2][1]
-            mid = 448
-            source = picked[2][lo]
-            nc.scalar.copy(by_rows(grouped[2][:, mid:hi, :]), by_planes(source[:, :, mid - lo : hi - lo]))
-            nc.vector.tensor_copy(by_rows(grouped[2][:, lo:mid, :]), by_planes(source[:, :, 0 : mid - lo]))
+        def interleave_long(lo, hi):
+            nc.scalar.copy(by_rows(grouped[2][:, lo:hi, :]), by_planes(picked_long[:, :, lo - P : hi - P]))
+
+        def interleave_short():
+            nc.vector.tensor_copy(by_rows(grouped[2][:, 0:P, :]), by_planes(picked_short))
 
         def quantize(a, lo, hi):
             nc.vector.quantize_mx(
@@ -161,53 +201,47 @@ def tile_list_heads_tm_hl_silu_kernel(tc, xT, w, wgt, b, offs, out):
             for t in range(ROW_TILES):
                 multiply(a, t)
 
-        def gather_plane(a, i):
-            for c in range(2):
-                gather(a, i, c)
-
-        for i in range(PACK):
-            gather_plane(0, i)
-        truncate_w(0)
-        interleave(0, 0)
-        interleave(0, 1)
-        gather_plane(1, 0)
-        mask_w(0)
-        gather_plane(1, 1)
-        subtract_w(0)
-        truncate_w(1)
-        gather_plane(1, 2)
-        mask_w(1)
-        quantize(0, 0, END)
-        multiply_all(0)
-        gather_plane(1, 3)
-        subtract_w(1)
-        truncate_w(2)
-        interleave(1, 0)
-        interleave(1, 1)
-
-        gather(2, 0, 0)
-        mask_w(2)
-        gather(2, 1, 0)
-        subtract_w(2)
-        gather(2, 2, 0)
-        gather(2, 3, 0)
-        interleave(2, 0)
-        quantize(1, 0, END)
-        multiply_all(1)
-        gather(2, 0, 1)
+        for h in range(2):
+            mask_words(hi_first[h][:], w_first[h][:])
+            weave_hi(0, hi_first[h][:], h * (N // 2))
+        for h in range(2):
+            subtract_words(0, w_first[h][:], hi_first[h][:], h * (N // 2))
+        split_w(1)
+        weave_minus_hi(1)
+        quantize(0, HI, END)
+        gather(picked[0], 0, 0, 0, PICKS)
+        gather(picked[0], 0, 1, 0, PICKS)
+        split_w(2)
+        weave_minus_hi(2)
+        quantize(1, HI, END)
+        gather(picked[0], 0, 2, 0, PICKS)
+        gather(picked[0], 0, 3, 0, PICKS)
+        interleave(0)
+        for i in range(3):
+            gather(picked[1], 1, i, 0, PICKS)
         quantize(2, HI, END)
-        gather(2, 1, 1)
-        gather(2, 2, 1)
-        quantize(2, 0, 256)
-        multiply(2, 0)
+        quantize(0, 0, HI)
+        multiply_all(0)
+        gather(picked[1], 1, 3, 0, PICKS)
+        interleave(1)
+        for i in range(3):
+            gather(picked_long, 2, i, P, PICKS)
+        quantize(1, 0, HI)
+        multiply_all(1)
+        gather(picked_long, 2, 3, P, PICKS)
+        interleave_long(P, 2 * P)
+        interleave_long(2 * P, PICKS)
+        for i in (3, 0, 1, 2):
+            gather(picked_short, 2, i, 0, P)
+        quantize(2, P, 2 * P)
         multiply(2, 1)
-        quantize(2, 256, 384)
-        multiply(2, 2)
-        gather(2, 3, 1)
-        finish(0)
-        interleave_last()
+        interleave_short()
         finish(1)
-        quantize(2, 384, 512)
+        quantize(2, 0, P)
+        multiply(2, 0)
+        quantize(2, 2 * P, PICKS)
+        multiply(2, 2)
         multiply(2, 3)
+        finish(0)
         finish(2)
         finish(3)

@@ -163,11 +163,12 @@ def tile_list_heads_tm_hl_silu_kernel(tc, xT, w, wgt, b, offs, out):
         def interleave(a):
             nc.scalar.copy(by_rows(grouped[a][:, 0:PICKS, :]), by_planes(picked[a][:]))
 
-        def interleave_long(lo, hi):
-            nc.scalar.copy(by_rows(grouped[2][:, lo:hi, :]), by_planes(picked_long[:, :, lo - P : hi - P]))
+        def interleave_long(u):
+            pair = slice(2 * u, 2 * u + 2)
+            nc.scalar.copy(by_rows(grouped[2][:, P:PICKS, pair]), by_planes(picked_long[:, pair, :]))
 
         def interleave_short():
-            nc.vector.tensor_copy(by_rows(grouped[2][:, 0:P, :]), by_planes(picked_short))
+            nc.scalar.copy(by_rows(grouped[2][:, 0:P, :]), by_planes(picked_short))
 
         def quantize(a, lo, hi):
             nc.vector.quantize_mx(
@@ -175,6 +176,8 @@ def tile_list_heads_tm_hl_silu_kernel(tc, xT, w, wgt, b, offs, out):
                 scales=scales[a][:, lo:hi],
                 in_=grouped[a][:, lo:hi, :].rearrange("p j i -> p (j i)"),
             )
+
+        first_pass = (0, 0, 1, 1)
 
         def multiply(a, t):
             rows = slice(t * P, (t + 1) * P)
@@ -186,7 +189,7 @@ def tile_list_heads_tm_hl_silu_kernel(tc, xT, w, wgt, b, offs, out):
                     lhsT_scale=scales[a][:, rows],
                     rhs=codes[a][:, cols].bitcast(FP8X4),
                     rhs_scale=scales[a][:, cols],
-                    start=(a == 0 and h == 0),
+                    start=(a == first_pass[t] and h == 0),
                     stop=(a == PASSES - 1 and h == 1),
                 )
 
@@ -221,27 +224,30 @@ def tile_list_heads_tm_hl_silu_kernel(tc, xT, w, wgt, b, offs, out):
             gather(picked[1], 1, i, 0, PICKS)
         quantize(2, HI, END)
         quantize(0, 0, HI)
-        multiply_all(0)
+        multiply(0, 0)
+        multiply(0, 1)
         gather(picked[1], 1, 3, 0, PICKS)
         interleave(1)
         for i in range(3):
             gather(picked_long, 2, i, P, PICKS)
+        interleave_long(0)
         quantize(1, 0, HI)
         multiply_all(1)
+        multiply(0, 2)
+        multiply(0, 3)
         gather(picked_long, 2, 3, P, PICKS)
-        interleave_long(P, 2 * P)
-        interleave_long(2 * P, PICKS)
+        interleave_long(1)
         for i in (3, 0, 1, 2):
             gather(picked_short, 2, i, 0, P)
-        quantize(2, P, 2 * P)
-        multiply(2, 1)
         interleave_short()
-        finish(1)
-        quantize(2, 0, P)
-        multiply(2, 0)
         quantize(2, 2 * P, PICKS)
         multiply(2, 2)
         multiply(2, 3)
-        finish(0)
+        quantize(2, P, 2 * P)
+        multiply(2, 1)
         finish(2)
+        quantize(2, 0, P)
+        multiply(2, 0)
         finish(3)
+        finish(1)
+        finish(0)

@@ -33,12 +33,13 @@ def tile_list_heads_tm_hl_silu_kernel(tc, xT, w, wgt, b, offs, out):
         keep = ctx.enter_context(tc.tile_pool(name="keep", bufs=1))
         psum = ctx.enter_context(tc.psum_pool(name="psum", bufs=1))
 
-        def held(shape, dtype, name):
-            return keep.tile(shape, dtype, name=name, align_bytes=64)
+        def held(shape, dtype, name, tag=None):
+            return keep.tile(shape, dtype, name=name, tag=tag or name, align_bytes=64)
 
         offsets = keep.tile([P, PICKS // 16], U16, name="offsets")
         weights = held([P, PICKS + P], F32, "weights")
         bias = held([P, N], F32, "bias")
+        bias_pairs = held([P, 2], F32, "bias_pairs")
         warm = held([P, 1], F32, "warm")
         planes = [[held([P, TOKENS], F32, f"plane{a}_{i}") for i in range(PACK)] for a in range(PASSES)]
         w_raw = {a: held([P, PACK, N], F32, f"w_raw{a}") for a in (1, 2)}
@@ -47,7 +48,8 @@ def tile_list_heads_tm_hl_silu_kernel(tc, xT, w, wgt, b, offs, out):
         minus_hi = {a: held([P, PACK, N], F32, f"minus_hi{a}") for a in (1, 2)}
         lo_turned = {a: [held([P, 2, P, 2], BF16, f"lo_turned{a}_{h}") for h in range(2)] for a in (1, 2)}
         identity = held([P, P], F32, "identity")
-        grouped = [held([P, PICKS + 2 * N, PACK], BF16, f"grouped{a}") for a in range(PASSES)]
+        grouped = {a: held([P, PICKS, PACK], BF16, f"grouped{a}") for a in (1, 2)}
+        grouped_w = {a: held([P, 2 * N, PACK], BF16, f"grouped_w{a}") for a in (0, 1)}
         codes = [held([P, PICKS + 2 * N], U32, f"codes{a}") for a in range(PASSES)]
         scales = [held([P, PICKS + 2 * N], U8, f"scales{a}") for a in range(PASSES)]
         sums = [psum.tile([P, 512], F32, name=f"sums{t}") for t in range(ROW_TILES)]
@@ -62,6 +64,7 @@ def tile_list_heads_tm_hl_silu_kernel(tc, xT, w, wgt, b, offs, out):
             )
 
         make_identity(nc, identity[:])
+        nc.scalar.dma_start(bias_pairs[:], b.rearrange("(p e) -> p e", e=2))
         nc.vector.memset(warm[:], 0.0)
         nc.scalar.activation(warm[:], warm[:], ACT.Silu)
 
@@ -81,7 +84,6 @@ def tile_list_heads_tm_hl_silu_kernel(tc, xT, w, wgt, b, offs, out):
         for a in (1, 2):
             for i in range(PACK):
                 load_plane(a, i)
-        nc.sync.dma_start(bias[:], b.partition_broadcast(P))
 
         HI, LO, END = PICKS, PICKS + N, PICKS + 2 * N
 
@@ -105,11 +107,11 @@ def tile_list_heads_tm_hl_silu_kernel(tc, xT, w, wgt, b, offs, out):
             return by_planes(words.bitcast(BF16)[:, :, 1 : 2 * width : 2])
 
         def weave_hi(a, hi, n0):
-            nc.scalar.copy(by_rows(grouped[a][:, HI + n0 : HI + n0 + hi.shape[2], :]), upper_halves(hi))
+            nc.scalar.copy(by_rows(grouped_w[a][:, n0 : n0 + hi.shape[2], :]), upper_halves(hi))
 
         def subtract_words(a, raw, hi, n0):
             nc.vector.tensor_tensor(
-                by_rows(grouped[a][:, LO + n0 : LO + n0 + hi.shape[2], :]), by_planes(raw), by_planes(hi), ALU.subtract
+                by_rows(grouped_w[a][:, N + n0 : N + n0 + hi.shape[2], :]), by_planes(raw), by_planes(hi), ALU.subtract
             )
 
         def split_w(a):
@@ -140,13 +142,14 @@ def tile_list_heads_tm_hl_silu_kernel(tc, xT, w, wgt, b, offs, out):
                 words = lo_turned[a][h][:].rearrange("n u p e -> n u (p e)").bitcast(F32)
                 for u in range(2):
                     nc.tensor.transpose(back[:, h, u, :], words[:, u, :], identity[:])
+            return back
+
+        def weave_w(a, back):
+            nc.scalar.activation(by_rows(grouped_w[a][:, 0:N, :]), upper_halves(minus_hi[a][:]), ACT.Copy, scale=-1.0)
             nc.scalar.copy(
-                grouped[a][:, LO:END, :].bitcast(F32).rearrange("p (h n) u -> p h n u", h=2),
+                grouped_w[a][:, N : 2 * N, :].bitcast(F32).rearrange("p (h n) u -> p h n u", h=2),
                 back[:].rearrange("p h u n -> p h n u"),
             )
-
-        def weave_minus_hi(a):
-            nc.scalar.activation(by_rows(grouped[a][:, HI:LO, :]), upper_halves(minus_hi[a][:]), ACT.Copy, scale=-1.0)
 
         picked = [held([P, PACK, PICKS], F32, f"picked{a}") for a in range(2)]
         picked_long = held([P, PACK, PICKS - P], F32, "picked_long")
@@ -169,6 +172,13 @@ def tile_list_heads_tm_hl_silu_kernel(tc, xT, w, wgt, b, offs, out):
 
         def interleave_short():
             nc.scalar.copy(by_rows(grouped[2][:, 0:P, :]), by_planes(picked_short))
+
+        def quantize_w(a):
+            nc.vector.quantize_mx(
+                out=codes[a][:, HI:END].bitcast(FP8X4),
+                scales=scales[a][:, HI:END],
+                in_=grouped_w[a][:].rearrange("p j i -> p (j i)"),
+            )
 
         def quantize(a, lo, hi):
             nc.vector.quantize_mx(
@@ -193,6 +203,12 @@ def tile_list_heads_tm_hl_silu_kernel(tc, xT, w, wgt, b, offs, out):
                     stop=(a == PASSES - 1 and h == 1),
                 )
 
+        def spread_bias():
+            spread = psum.tile([P, 2, P], F32, name="spread")
+            for e in range(2):
+                nc.tensor.transpose(spread[:, e, :], bias_pairs[:, e : e + 1].to_broadcast([P, P]), identity[:])
+            nc.scalar.copy(bias[:].rearrange("p (j e) -> p j e", e=2), spread[:].rearrange("p e j -> p j e"))
+
         def finish(t):
             shifted = keep.tile([P, N], F32, name=f"shifted{t}")
             nc.vector.tensor_tensor(shifted[:], sums[t][:, 0:N], bias[:], ALU.add)
@@ -204,32 +220,36 @@ def tile_list_heads_tm_hl_silu_kernel(tc, xT, w, wgt, b, offs, out):
             for t in range(ROW_TILES):
                 multiply(a, t)
 
+        spread_bias()
         for h in range(2):
             mask_words(hi_first[h][:], w_first[h][:])
             weave_hi(0, hi_first[h][:], h * (N // 2))
         for h in range(2):
             subtract_words(0, w_first[h][:], hi_first[h][:], h * (N // 2))
-        split_w(1)
-        weave_minus_hi(1)
-        quantize(0, HI, END)
+        weave_w(1, split_w(1))
+        quantize_w(0)
         gather(picked[0], 0, 0, 0, PICKS)
         gather(picked[0], 0, 1, 0, PICKS)
-        split_w(2)
-        weave_minus_hi(2)
-        quantize(1, HI, END)
+        back_last = split_w(2)
+        quantize_w(1)
         gather(picked[0], 0, 2, 0, PICKS)
         gather(picked[0], 0, 3, 0, PICKS)
+        gather(picked[1], 1, 0, 0, PICKS)
+        grouped[0] = held([P, PICKS, PACK], BF16, "grouped0", tag="plane1_0")
         interleave(0)
-        for i in range(3):
-            gather(picked[1], 1, i, 0, PICKS)
-        quantize(2, HI, END)
+        gather(picked[1], 1, 1, 0, PICKS)
+        gather(picked[1], 1, 2, 0, PICKS)
+        grouped_w[2] = held([P, 2 * N, PACK], BF16, "grouped_w2", tag="plane1_2")
+        weave_w(2, back_last)
+        gather(picked[1], 1, 3, 0, PICKS)
+        interleave(1)
         quantize(0, 0, HI)
         multiply(0, 0)
         multiply(0, 1)
-        gather(picked[1], 1, 3, 0, PICKS)
-        interleave(1)
-        for i in range(3):
-            gather(picked_long, 2, i, P, PICKS)
+        gather(picked_long, 2, 0, P, PICKS)
+        quantize_w(2)
+        gather(picked_long, 2, 1, P, PICKS)
+        gather(picked_long, 2, 2, P, PICKS)
         interleave_long(0)
         quantize(1, 0, HI)
         multiply_all(1)

@@ -78,9 +78,9 @@ def tile_list_heads_tm_hl_silu_kernel(tc, xT, w, wgt, b, offs, out):
         nc.sync.dma_start(weights[:, 0:PICKS], wgt)
         load_plane(0, 0)
         load_plane(0, 1)
-        load_w(2)
         load_plane(0, 2)
         load_plane(0, 3)
+        load_w(2)
         for a in (1, 2):
             for i in range(PACK):
                 load_plane(a, i)
@@ -230,10 +230,10 @@ def tile_list_heads_tm_hl_silu_kernel(tc, xT, w, wgt, b, offs, out):
         quantize_w(0)
         gather(picked[0], 0, 0, 0, PICKS)
         gather(picked[0], 0, 1, 0, PICKS)
-        back_last = split_w(2)
-        quantize_w(1)
         gather(picked[0], 0, 2, 0, PICKS)
+        quantize_w(1)
         gather(picked[0], 0, 3, 0, PICKS)
+        back_last = split_w(2)
         gather(picked[1], 1, 0, 0, PICKS)
         grouped[0] = held([P, PICKS, PACK], BF16, "grouped0", tag="plane1_0")
         interleave(0)

@@ -38,7 +38,6 @@ def tile_list_heads_tm_hl_silu_kernel(tc, xT, w, wgt, b, offs, out):
 
         offsets = keep.tile([P, PICKS // 16], U16, name="offsets")
         weights = held([P, PICKS + P], F32, "weights")
-        bias = held([P, N], F32, "bias")
         bias_pairs = held([P, 2], F32, "bias_pairs")
         warm = held([P, 1], F32, "warm")
         planes = [[held([P, TOKENS], F32, f"plane{a}_{i}") for i in range(PACK)] for a in range(PASSES)]
@@ -73,10 +72,10 @@ def tile_list_heads_tm_hl_silu_kernel(tc, xT, w, wgt, b, offs, out):
                 w_first[h][:],
                 w[0:K_PASS, h * (N // 2) : (h + 1) * (N // 2)].rearrange("(p i) n -> p i n", i=PACK),
             )
-        load_w(1)
         nc.sync.dma_start(offsets[:], offs)
         nc.sync.dma_start(weights[:, 0:PICKS], wgt)
         load_plane(0, 0)
+        load_w(1)
         load_plane(0, 1)
         load_plane(0, 2)
         load_plane(0, 3)
@@ -166,9 +165,12 @@ def tile_list_heads_tm_hl_silu_kernel(tc, xT, w, wgt, b, offs, out):
         def interleave(a):
             nc.scalar.copy(by_rows(grouped[a][:, 0:PICKS, :]), by_planes(picked[a][:]))
 
-        def interleave_long(u):
+        def interleave_pair(u):
             pair = slice(2 * u, 2 * u + 2)
-            nc.scalar.copy(by_rows(grouped[2][:, P:PICKS, pair]), by_planes(picked_long[:, pair, :]))
+            nc.scalar.copy(by_rows(grouped[2][:, P : 2 * P, pair]), by_planes(picked_long[:, pair, 0:P]))
+
+        def interleave_long():
+            nc.scalar.copy(by_rows(grouped[2][:, 2 * P : PICKS, :]), by_planes(picked_long[:, :, P : PICKS - P]))
 
         def interleave_short():
             nc.scalar.copy(by_rows(grouped[2][:, 0:P, :]), by_planes(picked_short))
@@ -204,10 +206,12 @@ def tile_list_heads_tm_hl_silu_kernel(tc, xT, w, wgt, b, offs, out):
                 )
 
         def spread_bias():
+            bias = held([P, N], F32, "bias", tag="w_first0")
             spread = psum.tile([P, 2, P], F32, name="spread")
             for e in range(2):
                 nc.tensor.transpose(spread[:, e, :], bias_pairs[:, e : e + 1].to_broadcast([P, P]), identity[:])
             nc.scalar.copy(bias[:].rearrange("p (j e) -> p j e", e=2), spread[:].rearrange("p e j -> p j e"))
+            return bias
 
         def finish(t):
             shifted = keep.tile([P, N], F32, name=f"shifted{t}")
@@ -220,20 +224,20 @@ def tile_list_heads_tm_hl_silu_kernel(tc, xT, w, wgt, b, offs, out):
             for t in range(ROW_TILES):
                 multiply(a, t)
 
-        spread_bias()
         for h in range(2):
             mask_words(hi_first[h][:], w_first[h][:])
             weave_hi(0, hi_first[h][:], h * (N // 2))
         for h in range(2):
             subtract_words(0, w_first[h][:], hi_first[h][:], h * (N // 2))
-        weave_w(1, split_w(1))
         quantize_w(0)
         gather(picked[0], 0, 0, 0, PICKS)
+        bias = spread_bias()
+        weave_w(1, split_w(1))
         gather(picked[0], 0, 1, 0, PICKS)
         gather(picked[0], 0, 2, 0, PICKS)
-        quantize_w(1)
         gather(picked[0], 0, 3, 0, PICKS)
         back_last = split_w(2)
+        quantize_w(1)
         gather(picked[1], 1, 0, 0, PICKS)
         grouped[0] = held([P, PICKS, PACK], BF16, "grouped0", tag="plane1_0")
         interleave(0)
@@ -250,13 +254,14 @@ def tile_list_heads_tm_hl_silu_kernel(tc, xT, w, wgt, b, offs, out):
         quantize_w(2)
         gather(picked_long, 2, 1, P, PICKS)
         gather(picked_long, 2, 2, P, PICKS)
-        interleave_long(0)
+        interleave_pair(0)
         quantize(1, 0, HI)
         multiply_all(1)
         multiply(0, 2)
         multiply(0, 3)
         gather(picked_long, 2, 3, P, PICKS)
-        interleave_long(1)
+        interleave_long()
+        interleave_pair(1)
         for i in (3, 0, 1, 2):
             gather(picked_short, 2, i, 0, P)
         interleave_short()

@@ -41,9 +41,8 @@ def tile_list_heads_tm_hl_silu_kernel(tc, xT, w, wgt, b, offs, out):
         bias_pairs = held([P, 2], F32, "bias_pairs")
         warm = held([P, 1], F32, "warm")
         planes = [[held([P, TOKENS], F32, f"plane{a}_{i}") for i in range(PACK)] for a in range(PASSES)]
-        w_raw = {a: held([P, PACK, N], F32, f"w_raw{a}") for a in (1, 2)}
-        w_first = [held([P, PACK, N // 2], F32, f"w_first{h}") for h in range(2)]
-        hi_first = [held([P, PACK, N // 2], F32, f"hi_first{h}") for h in range(2)]
+        w_raw = {a: held([P, PACK, N], F32, f"w_raw{a}") for a in range(PASSES)}
+        hi_first = held([P, PACK, N], F32, "hi_first")
         minus_hi = {a: held([P, PACK, N], F32, f"minus_hi{a}") for a in (1, 2)}
         lo_turned = {a: [held([P, 2, P, 2], BF16, f"lo_turned{a}_{h}") for h in range(2)] for a in (1, 2)}
         identity = held([P, P], F32, "identity")
@@ -69,8 +68,8 @@ def tile_list_heads_tm_hl_silu_kernel(tc, xT, w, wgt, b, offs, out):
 
         for h in range(2):
             nc.sync.dma_start(
-                w_first[h][:],
-                w[0:K_PASS, h * (N // 2) : (h + 1) * (N // 2)].rearrange("(p i) n -> p i n", i=PACK),
+                w_raw[0][:, 2 * h : 2 * h + 2, :],
+                w[0:K_PASS, :].rearrange("(p i) n -> p i n", i=PACK)[:, 2 * h : 2 * h + 2, :],
             )
         nc.sync.dma_start(offsets[:], offs)
         nc.sync.dma_start(weights[:, 0:PICKS], wgt)
@@ -206,7 +205,7 @@ def tile_list_heads_tm_hl_silu_kernel(tc, xT, w, wgt, b, offs, out):
                 )
 
         def spread_bias():
-            bias = held([P, N], F32, "bias", tag="w_first0")
+            bias = held([P, N], F32, "bias", tag="hi_first")
             spread = psum.tile([P, 2, P], F32, name="spread")
             for e in range(2):
                 nc.tensor.transpose(spread[:, e, :], bias_pairs[:, e : e + 1].to_broadcast([P, P]), identity[:])
@@ -225,10 +224,9 @@ def tile_list_heads_tm_hl_silu_kernel(tc, xT, w, wgt, b, offs, out):
                 multiply(a, t)
 
         for h in range(2):
-            mask_words(hi_first[h][:], w_first[h][:])
-            weave_hi(0, hi_first[h][:], h * (N // 2))
-        for h in range(2):
-            subtract_words(0, w_first[h][:], hi_first[h][:], h * (N // 2))
+            mask_words(hi_first[:, 2 * h : 2 * h + 2, :], w_raw[0][:, 2 * h : 2 * h + 2, :])
+        weave_hi(0, hi_first[:], 0)
+        subtract_words(0, w_raw[0][:], hi_first[:], 0)
         quantize_w(0)
         gather(picked[0], 0, 0, 0, PICKS)
         bias = spread_bias()

@@ -37,7 +37,7 @@ def tile_list_heads_tm_hl_silu_kernel(tc, xT, w, wgt, b, offs, out):
             return keep.tile(shape, dtype, name=name, tag=tag or name, align_bytes=64)
 
         offsets = keep.tile([P, PICKS // 16], U16, name="offsets")
-        weights = held([P, PICKS + P], F32, "weights")
+        weights = held([P, PICKS], F32, "weights")
         bias_pairs = held([P, 2], F32, "bias_pairs")
         warm = held([P, 1], F32, "warm")
         planes = [[held([P, TOKENS], F32, f"plane{a}_{i}") for i in range(PACK)] for a in range(PASSES)]
@@ -63,7 +63,7 @@ def tile_list_heads_tm_hl_silu_kernel(tc, xT, w, wgt, b, offs, out):
 
         make_identity(nc, identity[:])
         nc.scalar.dma_start(bias_pairs[:], b.rearrange("(p e) -> p e", e=2))
-        nc.vector.memset(warm[:], 0.0)
+        nc.gpsimd.memset(warm[:], 0.0)
         nc.scalar.activation(warm[:], warm[:], ACT.Silu)
 
         for h in range(2):
@@ -72,7 +72,7 @@ def tile_list_heads_tm_hl_silu_kernel(tc, xT, w, wgt, b, offs, out):
                 w[0:K_PASS, :].rearrange("(p i) n -> p i n", i=PACK)[:, 2 * h : 2 * h + 2, :],
             )
         nc.sync.dma_start(offsets[:], offs)
-        nc.sync.dma_start(weights[:, 0:PICKS], wgt)
+        nc.sync.dma_start(weights[:], wgt)
         load_plane(0, 0)
         load_w(1)
         load_plane(0, 1)
@@ -149,30 +149,22 @@ def tile_list_heads_tm_hl_silu_kernel(tc, xT, w, wgt, b, offs, out):
                 back[:].rearrange("p h u n -> p h n u"),
             )
 
-        picked = [held([P, PACK, PICKS], F32, f"picked{a}") for a in range(2)]
-        picked_long = held([P, PACK, PICKS - P], F32, "picked_long")
-        picked_short = weights[:, P : PICKS + P].rearrange("p (i j) -> p i j", i=PACK)
+        picked = [held([P, PACK, PICKS], F32, f"picked{a}") for a in range(PASSES)]
 
         def gather(into, a, i, lo, hi):
             nc.vector.tensor_tensor(
-                into[:, i, :],
+                into[:, i, lo:hi],
                 planes[a][i][:].indirect(offsets[:, lo // 16 : hi // 16]),
                 weights[:, lo:hi],
                 ALU.mult,
             )
 
-        def interleave(a):
-            nc.scalar.copy(by_rows(grouped[a][:, 0:PICKS, :]), by_planes(picked[a][:]))
+        def interleave(a, lo, hi):
+            nc.scalar.copy(by_rows(grouped[a][:, lo:hi, :]), by_planes(picked[a][:, :, lo:hi]))
 
-        def interleave_pair(u):
+        def interleave_pair(u, lo, hi):
             pair = slice(2 * u, 2 * u + 2)
-            nc.scalar.copy(by_rows(grouped[2][:, P : 2 * P, pair]), by_planes(picked_long[:, pair, 0:P]))
-
-        def interleave_long():
-            nc.scalar.copy(by_rows(grouped[2][:, 2 * P : PICKS, :]), by_planes(picked_long[:, :, P : PICKS - P]))
-
-        def interleave_short():
-            nc.scalar.copy(by_rows(grouped[2][:, 0:P, :]), by_planes(picked_short))
+            nc.scalar.copy(by_rows(grouped[2][:, lo:hi, pair]), by_planes(picked[2][:, pair, lo:hi]))
 
         def quantize_w(a):
             nc.vector.quantize_mx(
@@ -219,15 +211,23 @@ def tile_list_heads_tm_hl_silu_kernel(tc, xT, w, wgt, b, offs, out):
             nc.scalar.activation(result[:], shifted[:], ACT.Silu)
             nc.sync.dma_start(out[t * P : (t + 1) * P, :], result[:])
 
-        def multiply_all(a):
-            for t in range(ROW_TILES):
-                multiply(a, t)
-
+        mask_words(hi_first[:, 0:2, :], w_raw[0][:, 0:2, :])
         for h in range(2):
-            mask_words(hi_first[:, 2 * h : 2 * h + 2, :], w_raw[0][:, 2 * h : 2 * h + 2, :])
-        weave_hi(0, hi_first[:], 0)
-        subtract_words(0, w_raw[0][:], hi_first[:], 0)
-        quantize_w(0)
+            cols = slice(h * P, (h + 1) * P)
+            nc.vector.tensor_scalar(
+                hi_first[:, 2:4, cols].bitcast(I32), w_raw[0][:, 2:4, cols].bitcast(I32), KEEP_HIGH_WORD, None, ALU.bitwise_and
+            )
+        for h in range(2):
+            cols = slice(h * P, (h + 1) * P)
+            weave_hi(0, hi_first[:, :, cols], h * P)
+            subtract_words(0, w_raw[0][:, :, cols], hi_first[:, :, cols], h * P)
+        for h in range(2):
+            cols = slice(PICKS + h * N, PICKS + (h + 1) * N)
+            nc.vector.quantize_mx(
+                out=codes[0][:, cols].bitcast(FP8X4),
+                scales=scales[0][:, cols],
+                in_=grouped_w[0][:, h * N : (h + 1) * N, :].rearrange("p j i -> p (j i)"),
+            )
         gather(picked[0], 0, 0, 0, PICKS)
         bias = spread_bias()
         weave_w(1, split_w(1))
@@ -238,39 +238,34 @@ def tile_list_heads_tm_hl_silu_kernel(tc, xT, w, wgt, b, offs, out):
         quantize_w(1)
         gather(picked[1], 1, 0, 0, PICKS)
         grouped[0] = held([P, PICKS, PACK], BF16, "grouped0", tag="plane1_0")
-        interleave(0)
+        interleave(0, 0, PICKS)
         gather(picked[1], 1, 1, 0, PICKS)
         gather(picked[1], 1, 2, 0, PICKS)
         grouped_w[2] = held([P, 2 * N, PACK], BF16, "grouped_w2", tag="plane1_2")
         weave_w(2, back_last)
         gather(picked[1], 1, 3, 0, PICKS)
-        interleave(1)
+        interleave(1, 2 * P, PICKS)
+        interleave(1, 0, 2 * P)
         quantize(0, 0, HI)
         multiply(0, 0)
         multiply(0, 1)
-        gather(picked_long, 2, 0, P, PICKS)
+        gather(picked[2], 2, 0, 0, PICKS)
         quantize_w(2)
-        gather(picked_long, 2, 1, P, PICKS)
-        gather(picked_long, 2, 2, P, PICKS)
-        interleave_pair(0)
-        quantize(1, 0, HI)
-        multiply_all(1)
-        multiply(0, 2)
-        multiply(0, 3)
-        gather(picked_long, 2, 3, P, PICKS)
-        interleave_long()
-        interleave_pair(1)
-        for i in (3, 0, 1, 2):
-            gather(picked_short, 2, i, 0, P)
-        interleave_short()
-        quantize(2, 2 * P, PICKS)
-        multiply(2, 2)
-        multiply(2, 3)
-        quantize(2, P, 2 * P)
-        multiply(2, 1)
-        finish(2)
-        quantize(2, 0, P)
-        multiply(2, 0)
-        finish(3)
-        finish(1)
-        finish(0)
+        gather(picked[2], 2, 1, 0, PICKS)
+        quantize(1, 2 * P, PICKS)
+        for a, t in ((1, 2), (1, 3), (0, 2), (0, 3)):
+            multiply(a, t)
+        interleave_pair(0, 0, PICKS)
+        gather(picked[2], 2, 2, 0, PICKS)
+        quantize(1, 0, 2 * P)
+        multiply(1, 1)
+        multiply(1, 0)
+        last_order = (2, 3, 1, 0)
+        for t in last_order:
+            gather(picked[2], 2, 3, t * P, (t + 1) * P)
+            interleave_pair(1, t * P, (t + 1) * P)
+        for t in last_order:
+            quantize(2, t * P, (t + 1) * P)
+            multiply(2, t)
+        for t in last_order:
+            finish(t)

@@ -1,7 +1,6 @@
 from contextlib import ExitStack
 
 import concourse.mybir as mybir
-from concourse.masks import make_identity
 
 K, N, TOKENS, PICKS = 1536, 256, 1024, 512
 FLOPS = 2 * 2 * K * N * PICKS
@@ -42,15 +41,15 @@ def tile_list_heads_tm_hl_silu_kernel(tc, xT, w, wgt, b, offs, out):
         warm = held([P, 1], F32, "warm")
         planes = [[held([P, TOKENS], F32, f"plane{a}_{i}") for i in range(PACK)] for a in range(PASSES)]
         w_raw = {a: held([P, PACK, N], F32, f"w_raw{a}") for a in range(PASSES)}
-        hi_first = held([P, PACK, N], F32, "hi_first")
-        minus_hi = {a: held([P, PACK, N], F32, f"minus_hi{a}") for a in (1, 2)}
-        lo_turned = {a: [held([P, 2, P, 2], BF16, f"lo_turned{a}_{h}") for h in range(2)] for a in (1, 2)}
+        minus_hi = {a: held([P, PACK, N], F32, f"minus_hi{a}") for a in range(PASSES)}
+        lo_turned = {}
         identity = held([P, P], F32, "identity")
         grouped = {a: held([P, PICKS, PACK], BF16, f"grouped{a}") for a in (1, 2)}
-        grouped_w = {a: held([P, 2 * N, PACK], BF16, f"grouped_w{a}") for a in (0, 1)}
+        first = {0: held([P, P + N, PACK], BF16, "first0")}
+        grouped_w = {a: held([P, 2 * N, PACK], BF16, f"grouped_w{a}") for a in (1, 2)}
         codes = [held([P, PICKS + 2 * N], U32, f"codes{a}") for a in range(PASSES)]
         scales = [held([P, PICKS + 2 * N], U8, f"scales{a}") for a in range(PASSES)]
-        sums = [psum.tile([P, 512], F32, name=f"sums{t}") for t in range(ROW_TILES)]
+        sums = {}
 
         def load_w(a):
             nc.sync.dma_start(w_raw[a][:], w[a * K_PASS : (a + 1) * K_PASS, :].rearrange("(p i) n -> p i n", i=PACK))
@@ -61,29 +60,37 @@ def tile_list_heads_tm_hl_silu_kernel(tc, xT, w, wgt, b, offs, out):
                 xT[a * K_PASS : (a + 1) * K_PASS, :].rearrange("(p i) t -> p i t", i=PACK)[:, i, :],
             )
 
-        make_identity(nc, identity[:])
+        ones = held([P, P], F32, "ones")
+        ramp = held([P, P], F32, "ramp")
+        turned = held([P, P], F32, "turned")
+        nc.vector.memset(warm[:], 0.0)
+        nc.vector.memset(ones[:], 1.0)
+        nc.vector.tensor_tensor_scan(ramp[:], ones[:], ones[:], -1.0, ALU.mult, ALU.add)
+        nc.vector.transpose(turned[:], ramp[:])
+        for q in range(4):
+            rows = slice(32 * q, 32 * (q + 1))
+            nc.vector.tensor_scalar(
+                identity[rows, :], ramp[rows, :], turned[rows, 32 * q : 32 * q + 1], None, ALU.is_equal
+            )
         nc.scalar.dma_start(bias_pairs[:], b.rearrange("(p e) -> p e", e=2))
-        nc.gpsimd.memset(warm[:], 0.0)
         nc.scalar.activation(warm[:], warm[:], ACT.Silu)
 
+        nc.sync.dma_start(offsets[:], offs)
         for h in range(2):
             nc.sync.dma_start(
                 w_raw[0][:, 2 * h : 2 * h + 2, :],
                 w[0:K_PASS, :].rearrange("(p i) n -> p i n", i=PACK)[:, 2 * h : 2 * h + 2, :],
             )
-        nc.sync.dma_start(offsets[:], offs)
         nc.sync.dma_start(weights[:], wgt)
-        load_plane(0, 0)
-        load_w(1)
-        load_plane(0, 1)
-        load_plane(0, 2)
-        load_plane(0, 3)
-        load_w(2)
-        for a in (1, 2):
+        for a in range(PASSES):
             for i in range(PACK):
                 load_plane(a, i)
+                if (a, i) == (1, 0):
+                    load_w(1)
+                if (a, i) == (1, 3):
+                    load_w(2)
 
-        HI, LO, END = PICKS, PICKS + N, PICKS + 2 * N
+        X_AT, HI_AT, LO_AT = (N, 0, 0), (PICKS + N, PICKS, PICKS), (0, PICKS + N, PICKS + N)
 
         def by_rows(interleaved):
             return interleaved.rearrange("p (c e) i -> p c i e", e=4)
@@ -91,63 +98,64 @@ def tile_list_heads_tm_hl_silu_kernel(tc, xT, w, wgt, b, offs, out):
         def by_planes(separate):
             return separate.rearrange("p i (c e) -> p c i e", e=4)
 
-        def mask_words(hi, raw):
-            nc.vector.tensor_scalar(
-                hi.rearrange("p i n -> p (i n)").bitcast(I32),
-                raw.rearrange("p i n -> p (i n)").bitcast(I32),
-                KEEP_HIGH_WORD,
-                None,
-                ALU.bitwise_and,
-            )
-
         def upper_halves(words):
             width = words.shape[2]
             return by_planes(words.bitcast(BF16)[:, :, 1 : 2 * width : 2])
 
-        def weave_hi(a, hi, n0):
-            nc.scalar.copy(by_rows(grouped_w[a][:, n0 : n0 + hi.shape[2], :]), upper_halves(hi))
+        def half(h):
+            return slice(h * P, (h + 1) * P)
 
-        def subtract_words(a, raw, hi, n0):
-            nc.vector.tensor_tensor(
-                by_rows(grouped_w[a][:, N + n0 : N + n0 + hi.shape[2], :]), by_planes(raw), by_planes(hi), ALU.subtract
+        def mask(minus, raw):
+            nc.vector.tensor_scalar(
+                minus.bitcast(I32), raw.bitcast(I32), KEEP_HIGH_WORD, SIGN_BIT, ALU.bitwise_and, ALU.bitwise_xor
             )
+
+        def turn(difference, rows, opens):
+            for i in range(PACK):
+                nc.tensor.matmul(
+                    difference[:, i, :],
+                    rows[i],
+                    identity[:],
+                    start=(opens and i == 0),
+                    stop=(not opens and i == PACK - 1),
+                    is_transpose=True,
+                )
+
+        def rows_of(source, h):
+            return [source[:, i, half(h)] for i in range(PACK)]
+
+        def round_turned(a, difference, h, tag=None):
+            lo_turned[a, h] = held([P, 2, P, 2], BF16, f"lo_turned{a}_{h}", tag=tag)
+            nc.scalar.copy(lo_turned[a, h][:], difference[:].rearrange("n (u e) p -> n u p e", e=2))
+
+        def turn_back(a, back, h):
+            words = lo_turned[a, h][:].rearrange("n u p e -> n u (p e)").bitcast(F32)
+            for u in range(2):
+                nc.tensor.transpose(back[:, u, :], words[:, u, :], identity[:])
+
+        def weave_hi(into, minus):
+            nc.scalar.activation(by_rows(into), upper_halves(minus), ACT.Copy, scale=-1.0)
 
         def split_w(a):
-            nc.vector.tensor_scalar(
-                minus_hi[a][:].rearrange("p i n -> p (i n)").bitcast(I32),
-                w_raw[a][:].rearrange("p i n -> p (i n)").bitcast(I32),
-                KEEP_HIGH_WORD,
-                SIGN_BIT,
-                ALU.bitwise_and,
-                ALU.bitwise_xor,
-            )
+            differences = [psum.tile([P, PACK, P], F32, name=f"difference{h}") for h in range(2)]
             for h in range(2):
-                cols = slice(h * P, (h + 1) * P)
-                difference = psum.tile([P, PACK, P], F32, name=f"difference{h}")
-                for i in range(PACK):
-                    for term, source in enumerate((w_raw[a], minus_hi[a])):
-                        nc.tensor.matmul(
-                            difference[:, i, :],
-                            source[:, i, cols],
-                            identity[:],
-                            start=(term == 0),
-                            stop=(term == 1),
-                            is_transpose=True,
-                        )
-                nc.scalar.copy(lo_turned[a][h][:], difference[:].rearrange("n (u e) p -> n u p e", e=2))
-            back = psum.tile([P, 2, 2, P], F32, name="back")
+                turn(differences[h], rows_of(w_raw[a], h), True)
+            mask(minus_hi[a][:].rearrange("p i n -> p (i n)"), w_raw[a][:].rearrange("p i n -> p (i n)"))
+            weave_hi(grouped_w[a][:, 0:N, :], minus_hi[a][:])
             for h in range(2):
-                words = lo_turned[a][h][:].rearrange("n u p e -> n u (p e)").bitcast(F32)
-                for u in range(2):
-                    nc.tensor.transpose(back[:, h, u, :], words[:, u, :], identity[:])
-            return back
+                turn(differences[h], rows_of(minus_hi[a], h), False)
+                round_turned(a, differences[h], h)
 
-        def weave_w(a, back):
-            nc.scalar.activation(by_rows(grouped_w[a][:, 0:N, :]), upper_halves(minus_hi[a][:]), ACT.Copy, scale=-1.0)
+        def weave_lo(a, h):
+            back = psum.tile([P, 2, P], F32, name=f"back{h}")
+            turn_back(a, back, h)
             nc.scalar.copy(
-                grouped_w[a][:, N : 2 * N, :].bitcast(F32).rearrange("p (h n) u -> p h n u", h=2),
-                back[:].rearrange("p h u n -> p h n u"),
+                grouped_w[a][:, N + h * P : N + (h + 1) * P, :].bitcast(F32), back[:].rearrange("p u n -> p n u")
             )
+
+        def clock(name, source):
+            mark = keep.tile([P, 1], source.dtype, name=name)
+            nc.gpsimd.tensor_copy(mark[:], source)
 
         picked = [held([P, PACK, PICKS], F32, f"picked{a}") for a in range(PASSES)]
 
@@ -166,11 +174,12 @@ def tile_list_heads_tm_hl_silu_kernel(tc, xT, w, wgt, b, offs, out):
             pair = slice(2 * u, 2 * u + 2)
             nc.scalar.copy(by_rows(grouped[2][:, lo:hi, pair]), by_planes(picked[2][:, pair, lo:hi]))
 
-        def quantize_w(a):
+        def quantize_w(a, source, start):
+            at = slice(start, start + source.shape[1])
             nc.vector.quantize_mx(
-                out=codes[a][:, HI:END].bitcast(FP8X4),
-                scales=scales[a][:, HI:END],
-                in_=grouped_w[a][:].rearrange("p j i -> p (j i)"),
+                out=codes[a][:, at].bitcast(FP8X4),
+                scales=scales[a][:, at],
+                in_=source.rearrange("p j i -> p (j i)"),
             )
 
         def quantize(a, lo, hi):
@@ -180,12 +189,13 @@ def tile_list_heads_tm_hl_silu_kernel(tc, xT, w, wgt, b, offs, out):
                 in_=grouped[a][:, lo:hi, :].rearrange("p j i -> p (j i)"),
             )
 
-        first_pass = (0, 0, 1, 1)
+        first_pass = (1, 1, 1, 1)
 
         def multiply(a, t):
-            rows = slice(t * P, (t + 1) * P)
+            rows = slice(X_AT[a] + t * P, X_AT[a] + (t + 1) * P)
             for h in range(2):
-                cols = slice(HI + h * N, LO + h * N)
+                at = (HI_AT, LO_AT)[h][a]
+                cols = slice(at, at + N)
                 nc.tensor.matmul_mx(
                     out=sums[t][:, 0:N],
                     lhsT=codes[a][:, rows].bitcast(FP8X4),
@@ -196,9 +206,14 @@ def tile_list_heads_tm_hl_silu_kernel(tc, xT, w, wgt, b, offs, out):
                     stop=(a == PASSES - 1 and h == 1),
                 )
 
+        def open_sum(t, bank):
+            sums[t] = psum.tile([P, 512], F32, name=f"sums{t}", tag=bank)
+            multiply(1, t)
+            multiply(0, t)
+
         def spread_bias():
-            bias = held([P, N], F32, "bias", tag="hi_first")
-            spread = psum.tile([P, 2, P], F32, name="spread")
+            bias = held([P, N], F32, "bias")
+            spread = psum.tile([P, 2, P], F32, name="back0")
             for e in range(2):
                 nc.tensor.transpose(spread[:, e, :], bias_pairs[:, e : e + 1].to_broadcast([P, P]), identity[:])
             nc.scalar.copy(bias[:].rearrange("p (j e) -> p j e", e=2), spread[:].rearrange("p e j -> p j e"))
@@ -211,59 +226,64 @@ def tile_list_heads_tm_hl_silu_kernel(tc, xT, w, wgt, b, offs, out):
             nc.scalar.activation(result[:], shifted[:], ACT.Silu)
             nc.sync.dma_start(out[t * P : (t + 1) * P, :], result[:])
 
-        mask_words(hi_first[:, 0:2, :], w_raw[0][:, 0:2, :])
+        difference = psum.tile([P, PACK, P], F32, name="difference1")
+        turn(difference, rows_of(w_raw[0], 1), True)
+        early_hi = held([P, P, PACK], BF16, "early_hi")
+        early_lo = held([P, P, PACK], BF16, "early_lo")
+        mask(minus_hi[0][:, 0:2, :], w_raw[0][:, 0:2, :])
+        weave_hi(early_hi[:, :, 0:2], minus_hi[0][:, 0:2, half(1)])
         for h in range(2):
-            cols = slice(h * P, (h + 1) * P)
-            nc.vector.tensor_scalar(
-                hi_first[:, 2:4, cols].bitcast(I32), w_raw[0][:, 2:4, cols].bitcast(I32), KEEP_HIGH_WORD, None, ALU.bitwise_and
-            )
-        for h in range(2):
-            cols = slice(h * P, (h + 1) * P)
-            weave_hi(0, hi_first[:, :, cols], h * P)
-            subtract_words(0, w_raw[0][:, :, cols], hi_first[:, :, cols], h * P)
-        for h in range(2):
-            cols = slice(PICKS + h * N, PICKS + (h + 1) * N)
-            nc.vector.quantize_mx(
-                out=codes[0][:, cols].bitcast(FP8X4),
-                scales=scales[0][:, cols],
-                in_=grouped_w[0][:, h * N : (h + 1) * N, :].rearrange("p j i -> p (j i)"),
-            )
-        gather(picked[0], 0, 0, 0, PICKS)
+            mask(minus_hi[0][:, 2:4, half(h)], w_raw[0][:, 2:4, half(h)])
+        weave_hi(early_hi[:, :, 2:4], minus_hi[0][:, 2:4, half(1)])
+        nc.vector.tensor_tensor(
+            by_rows(early_lo[:]), by_planes(w_raw[0][:, :, half(0)]), by_planes(minus_hi[0][:, :, half(0)]), ALU.add
+        )
+        turn(difference, rows_of(minus_hi[0], 1), False)
+        round_turned(0, difference, 1)
+        back_first = psum.tile([P, 2, P], F32, name="back1")
+        turn_back(0, back_first, 1)
+        nc.scalar.copy(first[0][:, 0:P, :].bitcast(F32), back_first[:].rearrange("p u n -> p n u"))
+        quantize_w(0, early_hi[:], HI_AT[0] + P)
+        quantize_w(0, early_lo[:], LO_AT[0])
+        first[1] = held([P, N + P, PACK], BF16, "first1", tag="early_hi")
+        weave_hi(first[1][:, N : N + P, :], minus_hi[0][:, :, half(0)])
         bias = spread_bias()
-        weave_w(1, split_w(1))
-        gather(picked[0], 0, 1, 0, PICKS)
-        gather(picked[0], 0, 2, 0, PICKS)
-        gather(picked[0], 0, 3, 0, PICKS)
-        back_last = split_w(2)
-        quantize_w(1)
+        for i in range(PACK - 1):
+            gather(picked[0], 0, i, 0, PICKS)
+        for lo in (2 * P, 0):
+            gather(picked[0], 0, 3, lo, lo + 2 * P)
+            into = first[1][:, 0:N, :] if lo else first[0][:, P : P + N, :]
+            nc.scalar.copy(by_rows(into), by_planes(picked[0][:, :, lo : lo + 2 * P]))
         gather(picked[1], 1, 0, 0, PICKS)
-        grouped[0] = held([P, PICKS, PACK], BF16, "grouped0", tag="plane1_0")
-        interleave(0, 0, PICKS)
+        quantize_w(0, first[1][:], PICKS)
+        split_w(1)
+        quantize_w(0, first[0][:], P)
+        weave_lo(1, 0)
+        weave_lo(1, 1)
         gather(picked[1], 1, 1, 0, PICKS)
         gather(picked[1], 1, 2, 0, PICKS)
-        grouped_w[2] = held([P, 2 * N, PACK], BF16, "grouped_w2", tag="plane1_2")
-        weave_w(2, back_last)
-        gather(picked[1], 1, 3, 0, PICKS)
-        interleave(1, 2 * P, PICKS)
-        interleave(1, 0, 2 * P)
-        quantize(0, 0, HI)
-        multiply(0, 0)
-        multiply(0, 1)
-        gather(picked[2], 2, 0, 0, PICKS)
-        quantize_w(2)
-        gather(picked[2], 2, 1, 0, PICKS)
+        for lo in (2 * P, 0):
+            gather(picked[1], 1, 3, lo, lo + 2 * P)
+            interleave(1, lo, lo + 2 * P)
+        quantize_w(1, grouped_w[1][:], HI_AT[1])
+        split_w(2)
         quantize(1, 2 * P, PICKS)
-        for a, t in ((1, 2), (1, 3), (0, 2), (0, 3)):
-            multiply(a, t)
-        interleave_pair(0, 0, PICKS)
-        gather(picked[2], 2, 2, 0, PICKS)
+        weave_lo(2, 0)
+        open_sum(3, "difference0")
+        gather(picked[2], 2, 0, 0, PICKS)
         quantize(1, 0, 2 * P)
-        multiply(1, 1)
-        multiply(1, 0)
+        gather(picked[2], 2, 1, 0, PICKS)
+        interleave_pair(0, 0, PICKS)
+        weave_lo(2, 1)
+        open_sum(2, "difference1")
+        open_sum(1, "back0")
+        open_sum(0, "back1")
+        gather(picked[2], 2, 2, 0, PICKS)
         last_order = (2, 3, 1, 0)
         for t in last_order:
             gather(picked[2], 2, 3, t * P, (t + 1) * P)
             interleave_pair(1, t * P, (t + 1) * P)
+        quantize_w(2, grouped_w[2][:], HI_AT[2])
         for t in last_order:
             quantize(2, t * P, (t + 1) * P)
             multiply(2, t)

@@ -1,6 +1,7 @@
 from contextlib import ExitStack
 
 import concourse.mybir as mybir
+from concourse.masks import make_identity
 
 K, N, TOKENS, PICKS = 1536, 256, 1024, 512
 FLOPS = 2 * 2 * K * N * PICKS
@@ -44,11 +45,17 @@ def tile_list_heads_tm_hl_silu_kernel(tc, xT, w, wgt, b, offs, out):
         minus_hi = {a: held([P, PACK, N], F32, f"minus_hi{a}") for a in range(PASSES)}
         lo_turned = {}
         identity = held([P, P], F32, "identity")
-        grouped = {a: held([P, PICKS, PACK], BF16, f"grouped{a}") for a in (1, 2)}
-        first = {0: held([P, P + N, PACK], BF16, "first0")}
+        grouped = {2: held([P, PICKS, PACK], BF16, "grouped2")}
+        first = {0: held([P, N, PACK], BF16, "first0")}
+        second = [held([P, P + N, PACK], BF16, "second0"), held([P, N, PACK], BF16, "second1")]
         grouped_w = {a: held([P, 2 * N, PACK], BF16, f"grouped_w{a}") for a in (1, 2)}
-        codes = [held([P, PICKS + 2 * N], U32, f"codes{a}") for a in range(PASSES)]
-        scales = [held([P, PICKS + 2 * N], U8, f"scales{a}") for a in range(PASSES)]
+        WIDTH = PICKS + 2 * N
+        codes_ahead = held([P, 2 * WIDTH], U32, "codes_ahead")
+        scales_ahead = held([P, 2 * WIDTH], U8, "scales_ahead")
+        codes_last = held([P, WIDTH], U32, "codes_last")
+        scales_last = held([P, WIDTH], U8, "scales_last")
+        codes = [codes_ahead, codes_ahead, codes_last]
+        scales = [scales_ahead, scales_ahead, scales_last]
         sums = {}
 
         def load_w(a):
@@ -60,37 +67,29 @@ def tile_list_heads_tm_hl_silu_kernel(tc, xT, w, wgt, b, offs, out):
                 xT[a * K_PASS : (a + 1) * K_PASS, :].rearrange("(p i) t -> p i t", i=PACK)[:, i, :],
             )
 
-        ones = held([P, P], F32, "ones")
-        ramp = held([P, P], F32, "ramp")
-        turned = held([P, P], F32, "turned")
-        nc.vector.memset(warm[:], 0.0)
-        nc.vector.memset(ones[:], 1.0)
-        nc.vector.tensor_tensor_scan(ramp[:], ones[:], ones[:], -1.0, ALU.mult, ALU.add)
-        nc.vector.transpose(turned[:], ramp[:])
-        for q in range(4):
-            rows = slice(32 * q, 32 * (q + 1))
-            nc.vector.tensor_scalar(
-                identity[rows, :], ramp[rows, :], turned[rows, 32 * q : 32 * q + 1], None, ALU.is_equal
-            )
-        nc.scalar.dma_start(bias_pairs[:], b.rearrange("(p e) -> p e", e=2))
+        make_identity(nc, identity[:])
+        nc.gpsimd.memset(warm[:], 0.0)
         nc.scalar.activation(warm[:], warm[:], ACT.Silu)
 
-        nc.sync.dma_start(offsets[:], offs)
         for h in range(2):
             nc.sync.dma_start(
                 w_raw[0][:, 2 * h : 2 * h + 2, :],
                 w[0:K_PASS, :].rearrange("(p i) n -> p i n", i=PACK)[:, 2 * h : 2 * h + 2, :],
             )
+        nc.sync.dma_start(offsets[:], offs)
         nc.sync.dma_start(weights[:], wgt)
         for a in range(PASSES):
             for i in range(PACK):
                 load_plane(a, i)
+                if (a, i) == (0, 0):
+                    nc.sync.dma_start(bias_pairs[:], b.rearrange("(p e) -> p e", e=2))
                 if (a, i) == (1, 0):
                     load_w(1)
                 if (a, i) == (1, 3):
                     load_w(2)
 
-        X_AT, HI_AT, LO_AT = (N, 0, 0), (PICKS + N, PICKS, PICKS), (0, PICKS + N, PICKS + N)
+        X_AT = ((0, P, 2 * P, 3 * P), (WIDTH + 2 * P, WIDTH + 3 * P, WIDTH, WIDTH + P), (0, P, 2 * P, 3 * P))
+        HI_AT, LO_AT = (PICKS, WIDTH + PICKS, PICKS), (PICKS + N, WIDTH + PICKS + N, PICKS + N)
 
         def by_rows(interleaved):
             return interleaved.rearrange("p (c e) i -> p c i e", e=4)
@@ -167,9 +166,6 @@ def tile_list_heads_tm_hl_silu_kernel(tc, xT, w, wgt, b, offs, out):
                 ALU.mult,
             )
 
-        def interleave(a, lo, hi):
-            nc.scalar.copy(by_rows(grouped[a][:, lo:hi, :]), by_planes(picked[a][:, :, lo:hi]))
-
         def interleave_pair(u, lo, hi):
             pair = slice(2 * u, 2 * u + 2)
             nc.scalar.copy(by_rows(grouped[2][:, lo:hi, pair]), by_planes(picked[2][:, pair, lo:hi]))
@@ -192,7 +188,7 @@ def tile_list_heads_tm_hl_silu_kernel(tc, xT, w, wgt, b, offs, out):
         first_pass = (1, 1, 1, 1)
 
         def multiply(a, t):
-            rows = slice(X_AT[a] + t * P, X_AT[a] + (t + 1) * P)
+            rows = slice(X_AT[a][t], X_AT[a][t] + P)
             for h in range(2):
                 at = (HI_AT, LO_AT)[h][a]
                 cols = slice(at, at + N)
@@ -242,7 +238,6 @@ def tile_list_heads_tm_hl_silu_kernel(tc, xT, w, wgt, b, offs, out):
         round_turned(0, difference, 1)
         back_first = psum.tile([P, 2, P], F32, name="back1")
         turn_back(0, back_first, 1)
-        nc.scalar.copy(first[0][:, 0:P, :].bitcast(F32), back_first[:].rearrange("p u n -> p n u"))
         quantize_w(0, early_hi[:], HI_AT[0] + P)
         quantize_w(0, early_lo[:], LO_AT[0])
         first[1] = held([P, N + P, PACK], BF16, "first1", tag="early_hi")
@@ -252,26 +247,28 @@ def tile_list_heads_tm_hl_silu_kernel(tc, xT, w, wgt, b, offs, out):
             gather(picked[0], 0, i, 0, PICKS)
         for lo in (2 * P, 0):
             gather(picked[0], 0, 3, lo, lo + 2 * P)
-            into = first[1][:, 0:N, :] if lo else first[0][:, P : P + N, :]
+            into = first[1][:, 0:N, :] if lo else first[0][:]
             nc.scalar.copy(by_rows(into), by_planes(picked[0][:, :, lo : lo + 2 * P]))
+        nc.scalar.copy(second[0][:, 0:P, :].bitcast(F32), back_first[:].rearrange("p u n -> p n u"))
         gather(picked[1], 1, 0, 0, PICKS)
-        quantize_w(0, first[1][:], PICKS)
+        quantize_w(0, first[1][:], N)
         split_w(1)
-        quantize_w(0, first[0][:], P)
+        quantize_w(0, first[0][:], 0)
         weave_lo(1, 0)
         weave_lo(1, 1)
         gather(picked[1], 1, 1, 0, PICKS)
         gather(picked[1], 1, 2, 0, PICKS)
         for lo in (2 * P, 0):
             gather(picked[1], 1, 3, lo, lo + 2 * P)
-            interleave(1, lo, lo + 2 * P)
+            into = second[0][:, P : P + N, :] if lo else second[1][:]
+            nc.scalar.copy(by_rows(into), by_planes(picked[1][:, :, lo : lo + 2 * P]))
         quantize_w(1, grouped_w[1][:], HI_AT[1])
         split_w(2)
-        quantize(1, 2 * P, PICKS)
+        quantize_w(1, second[0][:], WIDTH - P)
         weave_lo(2, 0)
         open_sum(3, "difference0")
         gather(picked[2], 2, 0, 0, PICKS)
-        quantize(1, 0, 2 * P)
+        quantize_w(1, second[1][:], WIDTH + N)
         gather(picked[2], 2, 1, 0, PICKS)
         interleave_pair(0, 0, PICKS)
         weave_lo(2, 1)

@@ -279,10 +279,12 @@ def tile_list_heads_tm_hl_silu_kernel(tc, xT, w, wgt, b, offs, out):
         last_order = (2, 3, 1, 0)
         for t in last_order:
             gather(picked[2], 2, 3, t * P, (t + 1) * P)
-            interleave_pair(1, t * P, (t + 1) * P)
+            if t:
+                interleave_pair(1, t * P, (t + 1) * P)
         quantize_w(2, grouped_w[2][:], HI_AT[2])
-        for t in last_order:
+        nc.vector.tensor_copy(by_rows(grouped[2][:, 0:P, 2:4]), by_planes(picked[2][:, 2:4, 0:P]))
+        for t in (2, 3, 0, 1):
             quantize(2, t * P, (t + 1) * P)
             multiply(2, t)
-        for t in last_order:
+        for t in (2, 3, 0, 1):
             finish(t)

@@ -20,10 +20,20 @@ P = 128
 PACK = 4
 K_PASS = P * PACK
 PASSES = K // K_PASS
-ROW_TILES = PICKS // P
+HALF_PICKS = PICKS // 2
+LIST_ROWS = 16
+RUN = 4
+BANK = 512
+WIDTH = PICKS + 2 * N
 
-KEEP_HIGH_WORD = -0x00100000
+KEEP_HIGH_BITS = -0x00100000
 SIGN_BIT = -0x80000000
+
+PICKS_AT = ((0, P, 2 * P, 3 * P), (WIDTH + 2 * P, WIDTH + 3 * P, WIDTH, WIDTH + P), (0, P, 2 * P, 3 * P))
+HI_AT = (PICKS, WIDTH + PICKS, PICKS)
+LO_AT = (PICKS + N, WIDTH + PICKS + N, PICKS + N)
+
+LAST_ORDER = (2, 3, 1, 0)
 
 
 def tile_list_heads_tm_hl_silu_kernel(tc, xT, w, wgt, b, offs, out):
@@ -36,141 +46,126 @@ def tile_list_heads_tm_hl_silu_kernel(tc, xT, w, wgt, b, offs, out):
         def held(shape, dtype, name, tag=None):
             return keep.tile(shape, dtype, name=name, tag=tag or name, align_bytes=64)
 
-        offsets = keep.tile([P, PICKS // 16], U16, name="offsets")
+        offsets = keep.tile([P, PICKS // LIST_ROWS], U16, name="offsets")
         weights = held([P, PICKS], F32, "weights")
         bias_pairs = held([P, 2], F32, "bias_pairs")
         warm = held([P, 1], F32, "warm")
         planes = [[held([P, TOKENS], F32, f"plane{a}_{i}") for i in range(PACK)] for a in range(PASSES)]
-        w_raw = {a: held([P, PACK, N], F32, f"w_raw{a}") for a in range(PASSES)}
-        minus_hi = {a: held([P, PACK, N], F32, f"minus_hi{a}") for a in range(PASSES)}
-        lo_turned = {}
+        w_raw = [held([P, PACK, N], F32, f"w_raw{a}") for a in range(PASSES)]
+        minus_hi = [held([P, PACK, N], F32, f"minus_hi{a}") for a in range(PASSES)]
         identity = held([P, P], F32, "identity")
-        grouped = {2: held([P, PICKS, PACK], BF16, "grouped2")}
-        first = {0: held([P, N, PACK], BF16, "first0")}
-        second = [held([P, P + N, PACK], BF16, "second0"), held([P, N, PACK], BF16, "second1")]
-        grouped_w = {a: held([P, 2 * N, PACK], BF16, f"grouped_w{a}") for a in (1, 2)}
-        WIDTH = PICKS + 2 * N
+        last_picks = held([P, PICKS, PACK], BF16, "grouped2")
+        lower0 = held([P, HALF_PICKS, PACK], BF16, "first0")
+        upper1 = held([P, P + HALF_PICKS, PACK], BF16, "second0")
+        lower1 = held([P, HALF_PICKS, PACK], BF16, "second1")
+        woven_w = {a: held([P, 2 * N, PACK], BF16, f"grouped_w{a}") for a in (1, 2)}
         codes_ahead = held([P, 2 * WIDTH], U32, "codes_ahead")
         scales_ahead = held([P, 2 * WIDTH], U8, "scales_ahead")
         codes_last = held([P, WIDTH], U32, "codes_last")
         scales_last = held([P, WIDTH], U8, "scales_last")
-        codes = [codes_ahead, codes_ahead, codes_last]
-        scales = [scales_ahead, scales_ahead, scales_last]
+        codes = (codes_ahead, codes_ahead, codes_last)
+        scales = (scales_ahead, scales_ahead, scales_last)
+        lo_turned = {}
         sums = {}
 
-        def load_w(a):
-            nc.sync.dma_start(w_raw[a][:], w[a * K_PASS : (a + 1) * K_PASS, :].rearrange("(p i) n -> p i n", i=PACK))
-
-        def load_plane(a, i):
-            nc.sync.dma_start(
-                planes[a][i][:],
-                xT[a * K_PASS : (a + 1) * K_PASS, :].rearrange("(p i) t -> p i t", i=PACK)[:, i, :],
-            )
+        def rows_of_pass(matrix, a):
+            return matrix[a * K_PASS : (a + 1) * K_PASS, :].rearrange("(p i) c -> p i c", i=PACK)
 
         make_identity(nc, identity[:])
         nc.gpsimd.memset(warm[:], 0.0)
         nc.scalar.activation(warm[:], warm[:], ACT.Silu)
 
-        for h in range(2):
-            nc.sync.dma_start(
-                w_raw[0][:, 2 * h : 2 * h + 2, :],
-                w[0:K_PASS, :].rearrange("(p i) n -> p i n", i=PACK)[:, 2 * h : 2 * h + 2, :],
-            )
+        for u in range(2):
+            pair = slice(2 * u, 2 * u + 2)
+            nc.sync.dma_start(w_raw[0][:, pair, :], rows_of_pass(w, 0)[:, pair, :])
         nc.sync.dma_start(offsets[:], offs)
         nc.sync.dma_start(weights[:], wgt)
+        w_behind_plane = {(1, 0): 1, (1, PACK - 1): 2}
         for a in range(PASSES):
             for i in range(PACK):
-                load_plane(a, i)
+                nc.sync.dma_start(planes[a][i][:], rows_of_pass(xT, a)[:, i, :])
                 if (a, i) == (0, 0):
                     nc.sync.dma_start(bias_pairs[:], b.rearrange("(p e) -> p e", e=2))
-                if (a, i) == (1, 0):
-                    load_w(1)
-                if (a, i) == (1, 3):
-                    load_w(2)
-
-        X_AT = ((0, P, 2 * P, 3 * P), (WIDTH + 2 * P, WIDTH + 3 * P, WIDTH, WIDTH + P), (0, P, 2 * P, 3 * P))
-        HI_AT, LO_AT = (PICKS, WIDTH + PICKS, PICKS), (PICKS + N, WIDTH + PICKS + N, PICKS + N)
+                if (a, i) in w_behind_plane:
+                    later = w_behind_plane[a, i]
+                    nc.sync.dma_start(w_raw[later][:], rows_of_pass(w, later))
 
         def by_rows(interleaved):
-            return interleaved.rearrange("p (c e) i -> p c i e", e=4)
+            return interleaved.rearrange("p (c e) i -> p c i e", e=RUN)
 
         def by_planes(separate):
-            return separate.rearrange("p i (c e) -> p c i e", e=4)
-
-        def upper_halves(words):
-            width = words.shape[2]
-            return by_planes(words.bitcast(BF16)[:, :, 1 : 2 * width : 2])
+            return separate.rearrange("p i (c e) -> p c i e", e=RUN)
 
         def half(h):
             return slice(h * P, (h + 1) * P)
 
         def mask(minus, raw):
             nc.vector.tensor_scalar(
-                minus.bitcast(I32), raw.bitcast(I32), KEEP_HIGH_WORD, SIGN_BIT, ALU.bitwise_and, ALU.bitwise_xor
+                minus.bitcast(I32), raw.bitcast(I32), KEEP_HIGH_BITS, SIGN_BIT, ALU.bitwise_and, ALU.bitwise_xor
             )
 
-        def turn(difference, rows, opens):
+        def turn(difference, source, h, opens):
             for i in range(PACK):
                 nc.tensor.matmul(
                     difference[:, i, :],
-                    rows[i],
+                    source[:, i, half(h)],
                     identity[:],
                     start=(opens and i == 0),
                     stop=(not opens and i == PACK - 1),
                     is_transpose=True,
                 )
 
-        def rows_of(source, h):
-            return [source[:, i, half(h)] for i in range(PACK)]
-
-        def round_turned(a, difference, h, tag=None):
-            lo_turned[a, h] = held([P, 2, P, 2], BF16, f"lo_turned{a}_{h}", tag=tag)
+        def round_turned(a, difference, h):
+            lo_turned[a, h] = held([P, 2, P, 2], BF16, f"lo_turned{a}_{h}")
             nc.scalar.copy(lo_turned[a, h][:], difference[:].rearrange("n (u e) p -> n u p e", e=2))
 
-        def turn_back(a, back, h):
+        def turn_back(a, h):
+            back = psum.tile([P, 2, P], F32, name=f"back{h}")
             words = lo_turned[a, h][:].rearrange("n u p e -> n u (p e)").bitcast(F32)
             for u in range(2):
                 nc.tensor.transpose(back[:, u, :], words[:, u, :], identity[:])
+            return back
+
+        def weave_lo(into, back):
+            nc.scalar.copy(into.bitcast(F32), back[:].rearrange("p u n -> p n u"))
 
         def weave_hi(into, minus):
-            nc.scalar.activation(by_rows(into), upper_halves(minus), ACT.Copy, scale=-1.0)
+            upper_halves = minus.bitcast(BF16)[:, :, 1 : 2 * minus.shape[2] : 2]
+            nc.scalar.activation(by_rows(into), by_planes(upper_halves), ACT.Copy, scale=-1.0)
 
         def split_w(a):
             differences = [psum.tile([P, PACK, P], F32, name=f"difference{h}") for h in range(2)]
             for h in range(2):
-                turn(differences[h], rows_of(w_raw[a], h), True)
+                turn(differences[h], w_raw[a], h, True)
             mask(minus_hi[a][:].rearrange("p i n -> p (i n)"), w_raw[a][:].rearrange("p i n -> p (i n)"))
-            weave_hi(grouped_w[a][:, 0:N, :], minus_hi[a][:])
+            weave_hi(woven_w[a][:, 0:N, :], minus_hi[a][:])
             for h in range(2):
-                turn(differences[h], rows_of(minus_hi[a], h), False)
+                turn(differences[h], minus_hi[a], h, False)
                 round_turned(a, differences[h], h)
 
-        def weave_lo(a, h):
-            back = psum.tile([P, 2, P], F32, name=f"back{h}")
-            turn_back(a, back, h)
-            nc.scalar.copy(
-                grouped_w[a][:, N + h * P : N + (h + 1) * P, :].bitcast(F32), back[:].rearrange("p u n -> p n u")
-            )
-
-        def clock(name, source):
-            mark = keep.tile([P, 1], source.dtype, name=name)
-            nc.gpsimd.tensor_copy(mark[:], source)
+        def end_split(a, h):
+            weave_lo(woven_w[a][:, N + h * P : N + (h + 1) * P, :], turn_back(a, h))
 
         picked = [held([P, PACK, PICKS], F32, f"picked{a}") for a in range(PASSES)]
 
-        def gather(into, a, i, lo, hi):
+        def gather(a, i, lo=0, hi=PICKS):
             nc.vector.tensor_tensor(
-                into[:, i, lo:hi],
-                planes[a][i][:].indirect(offsets[:, lo // 16 : hi // 16]),
+                picked[a][:, i, lo:hi],
+                planes[a][i][:].indirect(offsets[:, lo // LIST_ROWS : hi // LIST_ROWS]),
                 weights[:, lo:hi],
                 ALU.mult,
             )
 
-        def interleave_pair(u, lo, hi):
-            pair = slice(2 * u, 2 * u + 2)
-            nc.scalar.copy(by_rows(grouped[2][:, lo:hi, pair]), by_planes(picked[2][:, pair, lo:hi]))
+        def gather_last_plane(a, upper, lower):
+            for lo, into in ((HALF_PICKS, upper), (0, lower)):
+                gather(a, PACK - 1, lo, lo + HALF_PICKS)
+                nc.scalar.copy(by_rows(into), by_planes(picked[a][:, :, lo : lo + HALF_PICKS]))
 
-        def quantize_w(a, source, start):
+        def pair_sides(u, lo, hi):
+            pair = slice(2 * u, 2 * u + 2)
+            return by_rows(last_picks[:, lo:hi, pair]), by_planes(picked[2][:, pair, lo:hi])
+
+        def quantize(a, source, start):
             at = slice(start, start + source.shape[1])
             nc.vector.quantize_mx(
                 out=codes[a][:, at].bitcast(FP8X4),
@@ -178,19 +173,9 @@ def tile_list_heads_tm_hl_silu_kernel(tc, xT, w, wgt, b, offs, out):
                 in_=source.rearrange("p j i -> p (j i)"),
             )
 
-        def quantize(a, lo, hi):
-            nc.vector.quantize_mx(
-                out=codes[a][:, lo:hi].bitcast(FP8X4),
-                scales=scales[a][:, lo:hi],
-                in_=grouped[a][:, lo:hi, :].rearrange("p j i -> p (j i)"),
-            )
-
-        first_pass = (1, 1, 1, 1)
-
         def multiply(a, t):
-            rows = slice(X_AT[a][t], X_AT[a][t] + P)
-            for h in range(2):
-                at = (HI_AT, LO_AT)[h][a]
+            rows = slice(PICKS_AT[a][t], PICKS_AT[a][t] + P)
+            for at in (HI_AT[a], LO_AT[a]):
                 cols = slice(at, at + N)
                 nc.tensor.matmul_mx(
                     out=sums[t][:, 0:N],
@@ -198,32 +183,32 @@ def tile_list_heads_tm_hl_silu_kernel(tc, xT, w, wgt, b, offs, out):
                     lhsT_scale=scales[a][:, rows],
                     rhs=codes[a][:, cols].bitcast(FP8X4),
                     rhs_scale=scales[a][:, cols],
-                    start=(a == first_pass[t] and h == 0),
-                    stop=(a == PASSES - 1 and h == 1),
+                    start=(a == 1 and at == HI_AT[a]),
+                    stop=(a == 2 and at == LO_AT[a]),
                 )
 
         def open_sum(t, bank):
-            sums[t] = psum.tile([P, 512], F32, name=f"sums{t}", tag=bank)
+            sums[t] = psum.tile([P, BANK], F32, name=f"sums{t}", tag=bank)
             multiply(1, t)
             multiply(0, t)
 
         def spread_bias():
-            bias = held([P, N], F32, "bias")
+            spread_out = held([P, N], F32, "bias")
             spread = psum.tile([P, 2, P], F32, name="back0")
             for e in range(2):
                 nc.tensor.transpose(spread[:, e, :], bias_pairs[:, e : e + 1].to_broadcast([P, P]), identity[:])
-            nc.scalar.copy(bias[:].rearrange("p (j e) -> p j e", e=2), spread[:].rearrange("p e j -> p j e"))
-            return bias
+            nc.scalar.copy(spread_out[:].rearrange("p (j e) -> p j e", e=2), spread[:].rearrange("p e j -> p j e"))
+            return spread_out
 
         def finish(t):
             shifted = keep.tile([P, N], F32, name=f"shifted{t}")
             nc.vector.tensor_tensor(shifted[:], sums[t][:, 0:N], bias[:], ALU.add)
             result = keep.tile([P, N], F32, name=f"result{t}")
             nc.scalar.activation(result[:], shifted[:], ACT.Silu)
-            nc.sync.dma_start(out[t * P : (t + 1) * P, :], result[:])
+            nc.sync.dma_start(out[half(t), :], result[:])
 
         difference = psum.tile([P, PACK, P], F32, name="difference1")
-        turn(difference, rows_of(w_raw[0], 1), True)
+        turn(difference, w_raw[0], 1, True)
         early_hi = held([P, P, PACK], BF16, "early_hi")
         early_lo = held([P, P, PACK], BF16, "early_lo")
         mask(minus_hi[0][:, 0:2, :], w_raw[0][:, 0:2, :])
@@ -234,57 +219,54 @@ def tile_list_heads_tm_hl_silu_kernel(tc, xT, w, wgt, b, offs, out):
         nc.vector.tensor_tensor(
             by_rows(early_lo[:]), by_planes(w_raw[0][:, :, half(0)]), by_planes(minus_hi[0][:, :, half(0)]), ALU.add
         )
-        turn(difference, rows_of(minus_hi[0], 1), False)
+        turn(difference, minus_hi[0], 1, False)
         round_turned(0, difference, 1)
-        back_first = psum.tile([P, 2, P], F32, name="back1")
-        turn_back(0, back_first, 1)
-        quantize_w(0, early_hi[:], HI_AT[0] + P)
-        quantize_w(0, early_lo[:], LO_AT[0])
-        first[1] = held([P, N + P, PACK], BF16, "first1", tag="early_hi")
-        weave_hi(first[1][:, N : N + P, :], minus_hi[0][:, :, half(0)])
+        back_first = turn_back(0, 1)
+        quantize(0, early_hi[:], HI_AT[0] + P)
+        quantize(0, early_lo[:], LO_AT[0])
+        upper0 = held([P, HALF_PICKS + P, PACK], BF16, "first1", tag="early_hi")
+        weave_hi(upper0[:, HALF_PICKS : HALF_PICKS + P, :], minus_hi[0][:, :, half(0)])
         bias = spread_bias()
+
         for i in range(PACK - 1):
-            gather(picked[0], 0, i, 0, PICKS)
-        for lo in (2 * P, 0):
-            gather(picked[0], 0, 3, lo, lo + 2 * P)
-            into = first[1][:, 0:N, :] if lo else first[0][:]
-            nc.scalar.copy(by_rows(into), by_planes(picked[0][:, :, lo : lo + 2 * P]))
-        nc.scalar.copy(second[0][:, 0:P, :].bitcast(F32), back_first[:].rearrange("p u n -> p n u"))
-        gather(picked[1], 1, 0, 0, PICKS)
-        quantize_w(0, first[1][:], N)
+            gather(0, i)
+        gather_last_plane(0, upper0[:, 0:HALF_PICKS, :], lower0[:])
+        weave_lo(upper1[:, 0:P, :], back_first)
+        gather(1, 0)
+        quantize(0, upper0[:], PICKS_AT[0][2])
         split_w(1)
-        quantize_w(0, first[0][:], 0)
-        weave_lo(1, 0)
-        weave_lo(1, 1)
-        gather(picked[1], 1, 1, 0, PICKS)
-        gather(picked[1], 1, 2, 0, PICKS)
-        for lo in (2 * P, 0):
-            gather(picked[1], 1, 3, lo, lo + 2 * P)
-            into = second[0][:, P : P + N, :] if lo else second[1][:]
-            nc.scalar.copy(by_rows(into), by_planes(picked[1][:, :, lo : lo + 2 * P]))
-        quantize_w(1, grouped_w[1][:], HI_AT[1])
+        quantize(0, lower0[:], PICKS_AT[0][0])
+        end_split(1, 0)
+        end_split(1, 1)
+
+        gather(1, 1)
+        gather(1, 2)
+        gather_last_plane(1, upper1[:, P : P + HALF_PICKS, :], lower1[:])
+        quantize(1, woven_w[1][:], HI_AT[1])
         split_w(2)
-        quantize_w(1, second[0][:], WIDTH - P)
-        weave_lo(2, 0)
+        quantize(1, upper1[:], LO_AT[0] + P)
+        end_split(2, 0)
         open_sum(3, "difference0")
-        gather(picked[2], 2, 0, 0, PICKS)
-        quantize_w(1, second[1][:], WIDTH + N)
-        gather(picked[2], 2, 1, 0, PICKS)
-        interleave_pair(0, 0, PICKS)
-        weave_lo(2, 1)
+
+        gather(2, 0)
+        quantize(1, lower1[:], PICKS_AT[1][0])
+        gather(2, 1)
+        nc.scalar.copy(*pair_sides(0, 0, PICKS))
+        end_split(2, 1)
         open_sum(2, "difference1")
         open_sum(1, "back0")
         open_sum(0, "back1")
-        gather(picked[2], 2, 2, 0, PICKS)
-        last_order = (2, 3, 1, 0)
-        for t in last_order:
-            gather(picked[2], 2, 3, t * P, (t + 1) * P)
-            if t:
-                interleave_pair(1, t * P, (t + 1) * P)
-        quantize_w(2, grouped_w[2][:], HI_AT[2])
-        nc.vector.tensor_copy(by_rows(grouped[2][:, 0:P, 2:4]), by_planes(picked[2][:, 2:4, 0:P]))
-        for t in (2, 3, 0, 1):
-            quantize(2, t * P, (t + 1) * P)
+        gather(2, 2)
+        for t in LAST_ORDER:
+            gather(2, PACK - 1, t * P, (t + 1) * P)
+            if t != LAST_ORDER[-1]:
+                nc.scalar.copy(*pair_sides(1, t * P, (t + 1) * P))
+        quantize(2, woven_w[2][:], HI_AT[2])
+        for t in LAST_ORDER:
+            if t == LAST_ORDER[-2]:
+                last = LAST_ORDER[-1]
+                nc.vector.tensor_copy(*pair_sides(1, last * P, (last + 1) * P))
+            quantize(2, last_picks[:, half(t), :], PICKS_AT[2][t])
             multiply(2, t)
-        for t in (2, 3, 0, 1):
+        for t in LAST_ORDER:
             finish(t)

from contextlib import ExitStack

import concourse.mybir as mybir
from concourse.masks import make_identity

K, N, TOKENS, PICKS = 1536, 256, 1024, 512
FLOPS = 2 * 2 * K * N * PICKS

F32 = mybir.dt.float32
BF16 = mybir.dt.bfloat16
I32 = mybir.dt.int32
U32 = mybir.dt.uint32
U16 = mybir.dt.uint16
U8 = mybir.dt.uint8
FP8X4 = mybir.dt.float8_e4m3fn_x4
ACT = mybir.ActivationFunctionType
ALU = mybir.AluOpType

P = 128
PACK = 4
K_PASS = P * PACK
PASSES = K // K_PASS
HALF_PICKS = PICKS // 2
LIST_ROWS = 16
RUN = 4
BANK = 512
WIDTH = PICKS + 2 * N

KEEP_HIGH_BITS = -0x00100000
SIGN_BIT = -0x80000000

PICKS_AT = ((0, P, 2 * P, 3 * P), (WIDTH + 2 * P, WIDTH + 3 * P, WIDTH, WIDTH + P), (0, P, 2 * P, 3 * P))
HI_AT = (PICKS, WIDTH + PICKS, PICKS)
LO_AT = (PICKS + N, WIDTH + PICKS + N, PICKS + N)

LAST_ORDER = (2, 3, 1, 0)


def tile_list_heads_tm_hl_silu_kernel(tc, xT, w, wgt, b, offs, out):
    nc = tc.nc

    with ExitStack() as ctx:
        keep = ctx.enter_context(tc.tile_pool(name="keep", bufs=1))
        psum = ctx.enter_context(tc.psum_pool(name="psum", bufs=1))

        def held(shape, dtype, name, tag=None):
            return keep.tile(shape, dtype, name=name, tag=tag or name, align_bytes=64)

        offsets = keep.tile([P, PICKS // LIST_ROWS], U16, name="offsets")
        weights = held([P, PICKS], F32, "weights")
        bias_pairs = held([P, 2], F32, "bias_pairs")
        warm = held([P, 1], F32, "warm")
        planes = [[held([P, TOKENS], F32, f"plane{a}_{i}") for i in range(PACK)] for a in range(PASSES)]
        w_raw = [held([P, PACK, N], F32, f"w_raw{a}") for a in range(PASSES)]
        minus_hi = [held([P, PACK, N], F32, f"minus_hi{a}") for a in range(PASSES)]
        identity = held([P, P], F32, "identity")
        last_picks = held([P, PICKS, PACK], BF16, "grouped2")
        lower0 = held([P, HALF_PICKS, PACK], BF16, "first0")
        upper1 = held([P, P + HALF_PICKS, PACK], BF16, "second0")
        lower1 = held([P, HALF_PICKS, PACK], BF16, "second1")
        woven_w = {a: held([P, 2 * N, PACK], BF16, f"grouped_w{a}") for a in (1, 2)}
        codes_ahead = held([P, 2 * WIDTH], U32, "codes_ahead")
        scales_ahead = held([P, 2 * WIDTH], U8, "scales_ahead")
        codes_last = held([P, WIDTH], U32, "codes_last")
        scales_last = held([P, WIDTH], U8, "scales_last")
        codes = (codes_ahead, codes_ahead, codes_last)
        scales = (scales_ahead, scales_ahead, scales_last)
        lo_turned = {}
        sums = {}

        def rows_of_pass(matrix, a):
            return matrix[a * K_PASS : (a + 1) * K_PASS, :].rearrange("(p i) c -> p i c", i=PACK)

        make_identity(nc, identity[:])
        nc.gpsimd.memset(warm[:], 0.0)
        nc.scalar.activation(warm[:], warm[:], ACT.Silu)

        for u in range(2):
            pair = slice(2 * u, 2 * u + 2)
            nc.sync.dma_start(w_raw[0][:, pair, :], rows_of_pass(w, 0)[:, pair, :])
        nc.sync.dma_start(offsets[:], offs)
        nc.sync.dma_start(weights[:], wgt)
        w_behind_plane = {(1, 0): 1, (1, PACK - 1): 2}
        for a in range(PASSES):
            for i in range(PACK):
                nc.sync.dma_start(planes[a][i][:], rows_of_pass(xT, a)[:, i, :])
                if (a, i) == (0, 0):
                    nc.sync.dma_start(bias_pairs[:], b.rearrange("(p e) -> p e", e=2))
                if (a, i) in w_behind_plane:
                    later = w_behind_plane[a, i]
                    nc.sync.dma_start(w_raw[later][:], rows_of_pass(w, later))

        def by_rows(interleaved):
            return interleaved.rearrange("p (c e) i -> p c i e", e=RUN)

        def by_planes(separate):
            return separate.rearrange("p i (c e) -> p c i e", e=RUN)

        def half(h):
            return slice(h * P, (h + 1) * P)

        def mask(minus, raw):
            nc.vector.tensor_scalar(
                minus.bitcast(I32), raw.bitcast(I32), KEEP_HIGH_BITS, SIGN_BIT, ALU.bitwise_and, ALU.bitwise_xor
            )

        def turn(difference, source, h, opens):
            for i in range(PACK):
                nc.tensor.matmul(
                    difference[:, i, :],
                    source[:, i, half(h)],
                    identity[:],
                    start=(opens and i == 0),
                    stop=(not opens and i == PACK - 1),
                    is_transpose=True,
                )

        def round_turned(a, difference, h):
            lo_turned[a, h] = held([P, 2, P, 2], BF16, f"lo_turned{a}_{h}")
            nc.scalar.copy(lo_turned[a, h][:], difference[:].rearrange("n (u e) p -> n u p e", e=2))

        def turn_back(a, h):
            back = psum.tile([P, 2, P], F32, name=f"back{h}")
            words = lo_turned[a, h][:].rearrange("n u p e -> n u (p e)").bitcast(F32)
            for u in range(2):
                nc.tensor.transpose(back[:, u, :], words[:, u, :], identity[:])
            return back

        def weave_lo(into, back):
            nc.scalar.copy(into.bitcast(F32), back[:].rearrange("p u n -> p n u"))

        def weave_hi(into, minus):
            upper_halves = minus.bitcast(BF16)[:, :, 1 : 2 * minus.shape[2] : 2]
            nc.scalar.activation(by_rows(into), by_planes(upper_halves), ACT.Copy, scale=-1.0)

        def split_w(a):
            differences = [psum.tile([P, PACK, P], F32, name=f"difference{h}") for h in range(2)]
            for h in range(2):
                turn(differences[h], w_raw[a], h, True)
            mask(minus_hi[a][:].rearrange("p i n -> p (i n)"), w_raw[a][:].rearrange("p i n -> p (i n)"))
            weave_hi(woven_w[a][:, 0:N, :], minus_hi[a][:])
            for h in range(2):
                turn(differences[h], minus_hi[a], h, False)
                round_turned(a, differences[h], h)

        def end_split(a, h):
            weave_lo(woven_w[a][:, N + h * P : N + (h + 1) * P, :], turn_back(a, h))

        picked = [held([P, PACK, PICKS], F32, f"picked{a}") for a in range(PASSES)]

        def gather(a, i, lo=0, hi=PICKS):
            nc.vector.tensor_tensor(
                picked[a][:, i, lo:hi],
                planes[a][i][:].indirect(offsets[:, lo // LIST_ROWS : hi // LIST_ROWS]),
                weights[:, lo:hi],
                ALU.mult,
            )

        def gather_last_plane(a, upper, lower):
            for lo, into in ((HALF_PICKS, upper), (0, lower)):
                gather(a, PACK - 1, lo, lo + HALF_PICKS)
                nc.scalar.copy(by_rows(into), by_planes(picked[a][:, :, lo : lo + HALF_PICKS]))

        def pair_sides(u, lo, hi):
            pair = slice(2 * u, 2 * u + 2)
            return by_rows(last_picks[:, lo:hi, pair]), by_planes(picked[2][:, pair, lo:hi])

        def quantize(a, source, start):
            at = slice(start, start + source.shape[1])
            nc.vector.quantize_mx(
                out=codes[a][:, at].bitcast(FP8X4),
                scales=scales[a][:, at],
                in_=source.rearrange("p j i -> p (j i)"),
            )

        def multiply(a, t):
            rows = slice(PICKS_AT[a][t], PICKS_AT[a][t] + P)
            for at in (HI_AT[a], LO_AT[a]):
                cols = slice(at, at + N)
                nc.tensor.matmul_mx(
                    out=sums[t][:, 0:N],
                    lhsT=codes[a][:, rows].bitcast(FP8X4),
                    lhsT_scale=scales[a][:, rows],
                    rhs=codes[a][:, cols].bitcast(FP8X4),
                    rhs_scale=scales[a][:, cols],
                    start=(a == 1 and at == HI_AT[a]),
                    stop=(a == 2 and at == LO_AT[a]),
                )

        def open_sum(t, bank):
            sums[t] = psum.tile([P, BANK], F32, name=f"sums{t}", tag=bank)
            multiply(1, t)
            multiply(0, t)

        def spread_bias():
            spread_out = held([P, N], F32, "bias")
            spread = psum.tile([P, 2, P], F32, name="back0")
            for e in range(2):
                nc.tensor.transpose(spread[:, e, :], bias_pairs[:, e : e + 1].to_broadcast([P, P]), identity[:])
            nc.scalar.copy(spread_out[:].rearrange("p (j e) -> p j e", e=2), spread[:].rearrange("p e j -> p j e"))
            return spread_out

        def finish(t):
            shifted = keep.tile([P, N], F32, name=f"shifted{t}")
            nc.vector.tensor_tensor(shifted[:], sums[t][:, 0:N], bias[:], ALU.add)
            result = keep.tile([P, N], F32, name=f"result{t}")
            nc.scalar.activation(result[:], shifted[:], ACT.Silu)
            nc.sync.dma_start(out[half(t), :], result[:])

        difference = psum.tile([P, PACK, P], F32, name="difference1")
        turn(difference, w_raw[0], 1, True)
        early_hi = held([P, P, PACK], BF16, "early_hi")
        early_lo = held([P, P, PACK], BF16, "early_lo")
        mask(minus_hi[0][:, 0:2, :], w_raw[0][:, 0:2, :])
        weave_hi(early_hi[:, :, 0:2], minus_hi[0][:, 0:2, half(1)])
        for h in range(2):
            mask(minus_hi[0][:, 2:4, half(h)], w_raw[0][:, 2:4, half(h)])
        weave_hi(early_hi[:, :, 2:4], minus_hi[0][:, 2:4, half(1)])
        nc.vector.tensor_tensor(
            by_rows(early_lo[:]), by_planes(w_raw[0][:, :, half(0)]), by_planes(minus_hi[0][:, :, half(0)]), ALU.add
        )
        turn(difference, minus_hi[0], 1, False)
        round_turned(0, difference, 1)
        back_first = turn_back(0, 1)
        quantize(0, early_hi[:], HI_AT[0] + P)
        quantize(0, early_lo[:], LO_AT[0])
        upper0 = held([P, HALF_PICKS + P, PACK], BF16, "first1", tag="early_hi")
        weave_hi(upper0[:, HALF_PICKS : HALF_PICKS + P, :], minus_hi[0][:, :, half(0)])
        bias = spread_bias()

        for i in range(PACK - 1):
            gather(0, i)
        gather_last_plane(0, upper0[:, 0:HALF_PICKS, :], lower0[:])
        weave_lo(upper1[:, 0:P, :], back_first)
        gather(1, 0)
        quantize(0, upper0[:], PICKS_AT[0][2])
        split_w(1)
        quantize(0, lower0[:], PICKS_AT[0][0])
        end_split(1, 0)
        end_split(1, 1)

        gather(1, 1)
        gather(1, 2)
        gather_last_plane(1, upper1[:, P : P + HALF_PICKS, :], lower1[:])
        quantize(1, woven_w[1][:], HI_AT[1])
        split_w(2)
        quantize(1, upper1[:], LO_AT[0] + P)
        end_split(2, 0)
        open_sum(3, "difference0")

        gather(2, 0)
        quantize(1, lower1[:], PICKS_AT[1][0])
        gather(2, 1)
        nc.scalar.copy(*pair_sides(0, 0, PICKS))
        end_split(2, 1)
        open_sum(2, "difference1")
        open_sum(1, "back0")
        open_sum(0, "back1")
        gather(2, 2)
        for t in LAST_ORDER:
            gather(2, PACK - 1, t * P, (t + 1) * P)
            if t != LAST_ORDER[-1]:
                nc.scalar.copy(*pair_sides(1, t * P, (t + 1) * P))
        quantize(2, woven_w[2][:], HI_AT[2])
        for t in LAST_ORDER:
            if t == LAST_ORDER[-2]:
                last = LAST_ORDER[-1]
                nc.vector.tensor_copy(*pair_sides(1, last * P, (last + 1) * P))
            quantize(2, last_picks[:, half(t), :], PICKS_AT[2][t])
            multiply(2, t)
        for t in LAST_ORDER:
            finish(t)
